import numpy as np
import ml_dtypes


def mxq(x, axis, fmt="e4m3"):
    dtype, down = {"e4m3": (ml_dtypes.float8_e4m3fn, 7), "e5m2": (ml_dtypes.float8_e5m2, 14)}[fmt]
    v = np.moveaxis(np.asarray(x, np.float32).astype(ml_dtypes.bfloat16).astype(np.float64), axis, -1)
    blocks = v.reshape(v.shape[:-1] + (-1, 32))
    amax = np.abs(blocks).max(-1, keepdims=True)
    byte = np.maximum(np.where(amax > 0, np.frexp(amax)[1] - 1 + 127, 0) - down, 1)
    scale = np.exp2(byte - 127.0)
    codes = (blocks / scale).astype(np.float32).astype(dtype).astype(np.float64)
    return np.moveaxis((codes * scale).reshape(v.shape), -1, axis)


WIDE = False


def mx_kscale(k):
    if not WIDE:
        return np.ones(k)
    levels = np.array([18, -18])
    if k % 512:
        return np.exp2(np.random.permutation(np.resize(levels, k // 32))).repeat(32)
    a = np.empty((k // 512, 16))
    for p in range(k // 512):
        a[p, :8] = np.random.permutation(np.resize(levels, 8))
        for g in range(8):
            far = levels[np.abs(levels - a[p, g]) >= 10]
            a[p, g + 8] = far[np.random.randint(len(far))]
    return np.exp2(a.ravel()).repeat(32)


def f64(x):
    return np.asarray(x).astype(np.float64)


def striped(idx):
    return np.tile(np.asarray(idx).reshape(-1, 16).T, (8, 1)).astype(np.uint16)


def unstriped(offs):
    return offs[:16].T.reshape(-1).astype(np.int64)


T, C, D, DV = 1024, 2048, 512, 512
BETA = 0.25


def setup_inputs():
    n = np.random.standard_normal
    grid = lambda v: np.clip(np.round(v * 16) / 16, -4, 4)
    u = mx_kscale(T)
    return {
        "zT": (grid(n((DV, T)))).astype(np.float32),
        "cb": (grid(n((DV, C)))).astype(np.float32),
        "tw": np.tile(np.random.randint(8, 33, T) / 16.0 * u, (128, 1)).astype(np.float32),
        "xT": (n((D, T)) / np.sqrt(T) / u).astype(np.float32),
        "offs": striped(np.random.randint(0, C, T)),
    }


def reference(zT, cb, tw, xT, offs):
    e = f64(zT) - f64(cb)[:, unstriped(offs)]
    g = f64(tw)[:1] * (BETA * e)
    return mxq(f64(xT), 1, "e4m3") @ mxq(g, 1, "e5m2").T

@@ -1,0 +1,292 @@
+from contextlib import ExitStack
+
+import concourse.mybir as mybir
+from concourse.masks import make_identity
+
+T, C, D, DV = 1024, 2048, 512, 512
+BETA = 0.25
+FLOPS = 2 * T * D * DV
+
+F32 = mybir.dt.float32
+BF16 = mybir.dt.bfloat16
+U32 = mybir.dt.uint32
+U16 = mybir.dt.uint16
+U8 = mybir.dt.uint8
+E4M3 = mybir.dt.float8_e4m3fn_x4
+E5M2 = mybir.dt.float8_e5m2_x4
+MULT = mybir.AluOpType.mult
+COPY = mybir.ActivationFunctionType.Copy
+
+P = 128
+PACK = 4
+K_PASS = P * PACK
+PASSES = T // K_PASS
+N_BLOCKS = DV // P
+D_BLOCKS = D // P
+LIST_COLS = K_PASS // 16
+
+
+def tile_attend_gvq_cw_w_kernel(tc, zT, cb, tw, xT, offs, out):
+    nc = tc.nc
+    with ExitStack() as ctx:
+        keep = ctx.enter_context(tc.tile_pool(name="keep", bufs=1))
+        psum = ctx.enter_context(tc.psum_pool(name="psum", bufs=8))
+
+        by_vector = ctx.enter_context(tc.tile_pool(name="by_vector", bufs=28))
+        by_scalar = ctx.enter_context(tc.tile_pool(name="by_scalar", bufs=16))
+
+        def result_tile(on_vector, shape, dtype):
+            pool = by_vector if on_vector else by_scalar
+            return pool.tile(shape, dtype, name="made", tag="made", align_bytes=64)
+
+        offsets = keep.tile([P, T // 16], U16, name="offsets")
+        cb_sb = [keep.tile([P, C], F32, name="cb%d" % b) for b in range(N_BLOCKS)]
+        z_sb = {}
+        x_sb = {}
+
+        def load_cb(b):
+            nc.sync.dma_start(cb_sb[b][:], cb[b * P : (b + 1) * P, :])
+
+        def load_rows(name, src, dst, b, g0, n):
+            rows = keep.tile([P, n * K_PASS], F32, name="%s%d_%d" % (name, b, g0))
+            nc.sync.dma_start(rows[:], src[b * P : (b + 1) * P, g0 * K_PASS : (g0 + n) * K_PASS])
+            for g in range(n):
+                dst[b, g0 + g] = rows[:, g * K_PASS : (g + 1) * K_PASS]
+
+        def load_z(b, g0, n):
+            load_rows("z", zT, z_sb, b, g0, n)
+
+        def load_x(j, g0, n):
+            load_rows("x", xT, x_sb, j, g0, n)
+
+        tw_sb = keep.tile([P, PASSES, 2 * PACK], F32, name="tw_sb")
+        nc.scalar.dma_start(tw_sb[:, :, 0:PACK], tw[0, :].rearrange("(g p t) -> p g t", g=PASSES, t=PACK))
+        nc.sync.dma_start(offsets[:], offs)
+        load_cb(0)
+        load_cb(1)
+        load_z(1, 0, 2)
+        load_cb(2)
+        load_z(0, 0, 2)
+        load_cb(3)
+        load_z(2, 0, 1)
+        load_z(2, 1, 1)
+        load_x(0, 0, 2)
+        load_z(3, 0, 1)
+        load_z(3, 1, 1)
+        load_x(1, 0, 2)
+        load_x(2, 0, 2)
+        load_x(3, 0, 2)
+
+        ident = keep.tile([P, P], F32, name="ident")
+        make_identity(nc, ident[:])
+        minus_one = keep.tile([P, K_PASS], F32, name="minus_one")
+        nc.vector.memset(minus_one[:], -1.0)
+        scale = keep.tile([P, PASSES, PACK], F32, name="scale")
+        nc.scalar.activation(scale[:], tw_sb[:, :, 0:PACK], COPY, scale=BETA)
+
+        g_bf = {}
+        g_codes = [keep.tile([P, DV], U32, name="g_codes%d" % g, align_bytes=64) for g in range(PASSES)]
+        g_scales = [keep.tile([P, DV], U8, name="g_scales%d" % g, align_bytes=64) for g in range(PASSES)]
+        neg_c = {}
+        g_pairs = {}
+        e_bank = {}
+        x_pairs = {}
+        x_bf = {}
+        x_codes = {}
+        x_scales = {}
+        acc = {}
+
+        def gather(b, g0, n):
+            picked = result_tile(True, [P, n * K_PASS], F32)
+            nc.vector.tensor_tensor(
+                picked[:],
+                cb_sb[b][:].indirect(offsets[:, g0 * LIST_COLS : (g0 + n) * LIST_COLS]),
+                minus_one[:, 0 : n * K_PASS],
+                MULT,
+            )
+            for g in range(n):
+                neg_c[b, g0 + g] = picked[:, g * K_PASS : (g + 1) * K_PASS]
+
+        def turn(src, b, g):
+            first = (b, g) not in e_bank
+            if first:
+                e_bank[b, g] = psum.tile([P, PACK, P], F32, name="bank", tag="bank")
+            for t in range(PACK):
+                nc.tensor.matmul(
+                    e_bank[b, g][:, t, :], lhsT=src[b, g][:, t:K_PASS:PACK], rhs=ident[:],
+                    is_transpose=True, start=(first and t == 0), stop=(not first and t == PACK - 1),
+                )
+
+        def weigh_vector(b, g):
+            g_bf[b, g] = result_tile(True, [P, P, PACK], BF16)
+            nc.vector.tensor_tensor(
+                g_bf[b, g][:],
+                e_bank[b, g][:].rearrange("p t n -> p n t"),
+                scale[:, g, :].unsqueeze(1).to_broadcast([P, P, PACK]),
+                MULT,
+            )
+
+        def weigh_act(b, g):
+            pairs = result_tile(False, [P, 2, P, 2], BF16)
+            for t in range(PACK):
+                nc.scalar.activation(
+                    pairs[:, t // 2, :, t % 2], e_bank[b, g][:, t, :], COPY, scale=scale[:, g, t : t + 1]
+                )
+            g_pairs[b, g] = pairs[:].rearrange("p u n e -> p (u n e)").bitcast(F32)
+
+        def interleave(b, g, n):
+            g_bf[b, g] = result_tile(True, [P, P, PACK], BF16)
+            dst = g_bf[b, g][:].rearrange("p n t -> p (n t)").bitcast(F32)
+            nc.vector.tensor_copy(
+                dst.rearrange("p (n u) -> p n u", u=2), g_pairs[b, g].rearrange("p (u n) -> p n u", u=2)
+            )
+
+        def quantize_g(g, b0, n):
+            cols = slice(b0 * P, (b0 + n) * P)
+            nc.vector.quantize_mx(
+                out=g_codes[g][:, cols].bitcast(E5M2),
+                scales=g_scales[g][:, cols],
+                in_=g_bf[b0, g][:].rearrange("p n t -> p (n t)"),
+            )
+
+        def cast_x(j, g, on_vector):
+            pairs = result_tile(on_vector, [P, 2, P, 2], BF16)
+            src = x_sb[j, g].rearrange("d (p u e) -> d u p e", u=2, e=2)
+            if on_vector:
+                nc.vector.tensor_copy(pairs[:], src)
+            else:
+                nc.scalar.copy(pairs[:], src)
+            x_pairs[j, g] = pairs[:].rearrange("d u p e -> d (u p e)").bitcast(F32)
+
+        def turn_x(j, g0, n, on_vector):
+            bank = psum.tile([P, n, 2, P], F32, name="bank", tag="bank")
+            for g in range(n):
+                for u in range(2):
+                    nc.tensor.transpose(bank[:, g, u, :], x_pairs[j, g0 + g][:, u * P : (u + 1) * P], ident[:])
+            grouped = result_tile(on_vector, [P, n * P * PACK], BF16)
+            dst = grouped[:].bitcast(F32).rearrange("p (g d u) -> p g d u", g=n, u=2)
+            src = bank[:].rearrange("p g u d -> p g d u")
+            if on_vector:
+                nc.vector.tensor_copy(dst, src)
+            else:
+                nc.scalar.copy(dst, src)
+            x_bf[j, g0] = grouped
+
+        def turn_x32(j, g, on_vector):
+            bank = psum.tile([P, PACK, P], F32, name="bank", tag="bank")
+            for t in range(PACK):
+                nc.tensor.transpose(bank[:, t, :], x_sb[j, g][:, t:K_PASS:PACK], ident[:])
+            grouped = result_tile(on_vector, [P, P * PACK], BF16)
+            dst = grouped[:].rearrange("p (d t) -> p d t", t=PACK)
+            src = bank[:].rearrange("p t d -> p d t")
+            if on_vector:
+                nc.vector.tensor_copy(dst, src)
+            else:
+                nc.scalar.copy(dst, src)
+            x_bf[j, g] = grouped
+
+        def quantize_x(j, g0, n):
+            codes = result_tile(True, [P, n * P], U32)
+            scales = keep.tile([P, n * P], U8, name="x_scales%d_%d" % (j, g0), align_bytes=64)
+            nc.vector.quantize_mx(out=codes[:].bitcast(E4M3), scales=scales[:], in_=x_bf[j, g0][:])
+            for g in range(n):
+                x_codes[j, g0 + g] = codes[:, g * P : (g + 1) * P]
+                x_scales[j, g0 + g] = scales[:, g * P : (g + 1) * P]
+
+        def product(j, g):
+            first = j not in acc
+            if first:
+                acc[j] = psum.tile([P, DV], F32, name="bank", tag="bank")
+            nc.tensor.matmul_mx(
+                out=acc[j][:], lhsT=x_codes[j, g].bitcast(E4M3), lhsT_scale=x_scales[j, g],
+                rhs=g_codes[g][:].bitcast(E5M2), rhs_scale=g_scales[g][:],
+                start=first, stop=not first,
+            )
+
+        def finish(j, on_vector, parts=1):
+            width = DV // parts
+            for h in range(parts):
+                cols = slice(h * width, (h + 1) * width)
+                result = result_tile(on_vector, [P, width], F32)
+                if on_vector:
+                    nc.vector.tensor_copy(result[:], acc[j][:, cols])
+                else:
+                    nc.scalar.copy(result[:], acc[j][:, cols])
+                nc.sync.dma_start(out[j * P : (j + 1) * P, cols], result[:])
+
+        gather(0, 0, 1)
+        turn(z_sb, 1, 1)
+        gather(0, 1, 1)
+        gather(1, 0, 1)
+        gather(1, 1, 1)
+        turn(z_sb, 1, 0)
+        gather(2, 0, 1)
+        turn(neg_c, 1, 0)
+        turn(z_sb, 0, 0)
+        gather(2, 1, 1)
+        turn(z_sb, 0, 1)
+        weigh_act(1, 0)
+        interleave(1, 0, 1)
+        turn(neg_c, 1, 1)
+        turn(z_sb, 2, 0)
+        gather(3, 0, 1)
+        turn(neg_c, 0, 0)
+        gather(3, 1, 1)
+        turn(neg_c, 2, 0)
+        weigh_act(0, 0)
+        weigh_act(1, 1)
+        interleave(0, 0, 1)
+        turn(neg_c, 2, 1)
+        turn(z_sb, 2, 1)
+        turn(neg_c, 0, 1)
+        interleave(1, 1, 1)
+        quantize_g(1, 1, 1)
+        turn(neg_c, 3, 1)
+        weigh_act(0, 1)
+        interleave(0, 1, 1)
+        weigh_vector(2, 0)
+        cast_x(1, 0, True)
+        turn(neg_c, 3, 0)
+        turn(z_sb, 3, 0)
+        weigh_act(2, 1)
+        cast_x(0, 1, False)
+        turn(z_sb, 3, 1)
+        interleave(2, 1, 1)
+        weigh_act(3, 0)
+        weigh_vector(3, 1)
+        turn_x32(1, 1, False)
+        turn_x(1, 0, 1, False)
+        quantize_g(0, 0, 1)
+        turn_x(0, 1, 1, True)
+        quantize_x(1, 0, 1)
+        quantize_x(0, 1, 1)
+        quantize_g(0, 1, 1)
+        quantize_g(1, 2, 1)
+        interleave(3, 0, 1)
+        turn_x32(0, 0, False)
+        quantize_x(0, 0, 1)
+        quantize_g(0, 3, 1)
+        quantize_x(1, 1, 1)
+        quantize_g(0, 2, 1)
+        turn_x32(2, 1, False)
+        turn_x32(2, 0, False)
+        turn_x32(3, 1, False)
+        turn_x32(3, 0, True)
+        quantize_x(2, 0, 1)
+        quantize_g(1, 0, 1)
+        quantize_g(1, 3, 1)
+        quantize_x(2, 1, 1)
+        quantize_x(3, 0, 1)
+        product(0, 1)
+        product(0, 0)
+        finish(0, False)
+        product(1, 1)
+        product(2, 0)
+        product(3, 0)
+        product(1, 0)
+        finish(1, False)
+        product(2, 1)
+        quantize_x(3, 1, 1)
+        finish(2, True)
+        product(3, 1)
+        finish(3, False)

@@ -32,8 +32,8 @@ def tile_attend_gvq_cw_w_kernel(tc, zT, cb, tw, xT, offs, out):
         keep = ctx.enter_context(tc.tile_pool(name="keep", bufs=1))
         psum = ctx.enter_context(tc.psum_pool(name="psum", bufs=8))
 
-        by_vector = ctx.enter_context(tc.tile_pool(name="by_vector", bufs=28))
-        by_scalar = ctx.enter_context(tc.tile_pool(name="by_scalar", bufs=16))
+        by_vector = ctx.enter_context(tc.tile_pool(name="by_vector", bufs=26))
+        by_scalar = ctx.enter_context(tc.tile_pool(name="by_scalar", bufs=17))
 
         def result_tile(on_vector, shape, dtype):
             pool = by_vector if on_vector else by_scalar
@@ -43,6 +43,7 @@ def tile_attend_gvq_cw_w_kernel(tc, zT, cb, tw, xT, offs, out):
         cb_sb = [keep.tile([P, C], F32, name="cb%d" % b) for b in range(N_BLOCKS)]
         z_sb = {}
         x_sb = {}
+        whole = {}
 
         def load_cb(b):
             nc.sync.dma_start(cb_sb[b][:], cb[b * P : (b + 1) * P, :])
@@ -50,6 +51,7 @@ def tile_attend_gvq_cw_w_kernel(tc, zT, cb, tw, xT, offs, out):
         def load_rows(name, src, dst, b, g0, n):
             rows = keep.tile([P, n * K_PASS], F32, name="%s%d_%d" % (name, b, g0))
             nc.sync.dma_start(rows[:], src[b * P : (b + 1) * P, g0 * K_PASS : (g0 + n) * K_PASS])
+            whole[name, b] = rows
             for g in range(n):
                 dst[b, g0 + g] = rows[:, g * K_PASS : (g + 1) * K_PASS]
 
@@ -63,19 +65,19 @@ def tile_attend_gvq_cw_w_kernel(tc, zT, cb, tw, xT, offs, out):
         nc.scalar.dma_start(tw_sb[:, :, 0:PACK], tw[0, :].rearrange("(g p t) -> p g t", g=PASSES, t=PACK))
         nc.sync.dma_start(offsets[:], offs)
         load_cb(0)
+        load_z(0, 0, 2)
         load_cb(1)
         load_z(1, 0, 2)
         load_cb(2)
-        load_z(0, 0, 2)
+        load_z(2, 0, 2)
         load_cb(3)
-        load_z(2, 0, 1)
-        load_z(2, 1, 1)
-        load_x(0, 0, 2)
         load_z(3, 0, 1)
         load_z(3, 1, 1)
+        load_x(0, 0, 2)
         load_x(1, 0, 2)
         load_x(2, 0, 2)
-        load_x(3, 0, 2)
+        load_x(3, 0, 1)
+        load_x(3, 1, 1)
 
         ident = keep.tile([P, P], F32, name="ident")
         make_identity(nc, ident[:])
@@ -156,13 +158,27 @@ def tile_attend_gvq_cw_w_kernel(tc, zT, cb, tw, xT, offs, out):
                 nc.vector.tensor_copy(pairs[:], src)
             else:
                 nc.scalar.copy(pairs[:], src)
-            x_pairs[j, g] = pairs[:].rearrange("d u p e -> d (u p e)").bitcast(F32)
+            words = pairs[:].rearrange("d u p e -> d (u p e)").bitcast(F32)
+            for u in range(2):
+                x_pairs[j, g, u] = words[:, u * P : (u + 1) * P]
+
+        def cast_both(j, on_vector):
+            pairs = result_tile(on_vector, [P, 2, PASSES * P, 2], BF16)
+            src = whole["x", j][:].rearrange("d (q u e) -> d u q e", u=2, e=2)
+            if on_vector:
+                nc.vector.tensor_copy(pairs[:], src)
+            else:
+                nc.scalar.copy(pairs[:], src)
+            words = pairs[:].rearrange("d u q e -> d (u q e)").bitcast(F32)
+            for u in range(2):
+                for g in range(PASSES):
+                    x_pairs[j, g, u] = words[:, (u * PASSES + g) * P : (u * PASSES + g + 1) * P]
 
         def turn_x(j, g0, n, on_vector):
             bank = psum.tile([P, n, 2, P], F32, name="bank", tag="bank")
             for g in range(n):
                 for u in range(2):
-                    nc.tensor.transpose(bank[:, g, u, :], x_pairs[j, g0 + g][:, u * P : (u + 1) * P], ident[:])
+                    nc.tensor.transpose(bank[:, g, u, :], x_pairs[j, g0 + g, u], ident[:])
             grouped = result_tile(on_vector, [P, n * P * PACK], BF16)
             dst = grouped[:].bitcast(F32).rearrange("p (g d u) -> p g d u", g=n, u=2)
             src = bank[:].rearrange("p g u d -> p g d u")
@@ -215,78 +231,77 @@ def tile_attend_gvq_cw_w_kernel(tc, zT, cb, tw, xT, offs, out):
                 nc.sync.dma_start(out[j * P : (j + 1) * P, cols], result[:])
 
         gather(0, 0, 1)
-        turn(z_sb, 1, 1)
-        gather(0, 1, 1)
-        gather(1, 0, 1)
-        gather(1, 1, 1)
-        turn(z_sb, 1, 0)
-        gather(2, 0, 1)
-        turn(neg_c, 1, 0)
         turn(z_sb, 0, 0)
-        gather(2, 1, 1)
-        turn(z_sb, 0, 1)
-        weigh_act(1, 0)
-        interleave(1, 0, 1)
-        turn(neg_c, 1, 1)
-        turn(z_sb, 2, 0)
-        gather(3, 0, 1)
         turn(neg_c, 0, 0)
-        gather(3, 1, 1)
-        turn(neg_c, 2, 0)
-        weigh_act(0, 0)
-        weigh_act(1, 1)
-        interleave(0, 0, 1)
-        turn(neg_c, 2, 1)
-        turn(z_sb, 2, 1)
+        gather(0, 1, 1)
+        turn(z_sb, 0, 1)
         turn(neg_c, 0, 1)
-        interleave(1, 1, 1)
-        quantize_g(1, 1, 1)
-        turn(neg_c, 3, 1)
+        weigh_act(0, 0)
         weigh_act(0, 1)
+        gather(1, 0, 1)
+        interleave(0, 0, 1)
+        turn(z_sb, 1, 0)
+        turn(neg_c, 1, 0)
+        gather(1, 1, 1)
         interleave(0, 1, 1)
-        weigh_vector(2, 0)
-        cast_x(1, 0, True)
-        turn(neg_c, 3, 0)
-        turn(z_sb, 3, 0)
-        weigh_act(2, 1)
-        cast_x(0, 1, False)
-        turn(z_sb, 3, 1)
-        interleave(2, 1, 1)
-        weigh_act(3, 0)
-        weigh_vector(3, 1)
-        turn_x32(1, 1, False)
-        turn_x(1, 0, 1, False)
+        turn(z_sb, 1, 1)
+        turn(neg_c, 1, 1)
         quantize_g(0, 0, 1)
-        turn_x(0, 1, 1, True)
-        quantize_x(1, 0, 1)
-        quantize_x(0, 1, 1)
-        quantize_g(0, 1, 1)
-        quantize_g(1, 2, 1)
-        interleave(3, 0, 1)
-        turn_x32(0, 0, False)
-        quantize_x(0, 0, 1)
-        quantize_g(0, 3, 1)
-        quantize_x(1, 1, 1)
-        quantize_g(0, 2, 1)
-        turn_x32(2, 1, False)
-        turn_x32(2, 0, False)
-        turn_x32(3, 1, False)
-        turn_x32(3, 0, True)
-        quantize_x(2, 0, 1)
         quantize_g(1, 0, 1)
-        quantize_g(1, 3, 1)
-        quantize_x(2, 1, 1)
-        quantize_x(3, 0, 1)
-        product(0, 1)
+        weigh_act(1, 0)
+        weigh_act(1, 1)
+        gather(2, 0, 1)
+        interleave(1, 0, 1)
+        turn(z_sb, 2, 0)
+        turn(neg_c, 2, 0)
+        gather(2, 1, 1)
+        interleave(1, 1, 1)
+        turn(z_sb, 2, 1)
+        turn(neg_c, 2, 1)
+        quantize_g(0, 1, 1)
+        quantize_g(1, 1, 1)
+        weigh_act(2, 0)
+        weigh_act(2, 1)
+        gather(3, 0, 1)
+        interleave(2, 0, 1)
+        turn(z_sb, 3, 0)
+        turn(neg_c, 3, 0)
+        gather(3, 1, 1)
+        interleave(2, 1, 1)
+        turn(z_sb, 3, 1)
+        turn(neg_c, 3, 1)
+        cast_both(0, False)
+        weigh_vector(3, 0)
+        cast_both(1, False)
+        turn_x(0, 0, 1, True)
+        turn_x(0, 1, 1, True)
+        quantize_x(0, 0, 1)
+        cast_both(2, False)
+        cast_x(3, 0, True)
+        weigh_vector(3, 1)
+        quantize_g(0, 2, 1)
+        cast_x(3, 1, False)
+        quantize_g(0, 3, 1)
+        turn_x(1, 0, 2, False)
+        quantize_x(0, 1, 1)
         product(0, 0)
-        finish(0, False)
-        product(1, 1)
+        turn_x(2, 1, 1, False)
+        quantize_g(1, 3, 1)
+        turn_x(2, 0, 1, True)
+        turn_x(3, 0, 2, False)
+        quantize_x(2, 0, 1)
+        quantize_x(2, 1, 1)
         product(2, 0)
-        product(3, 0)
+        quantize_g(1, 2, 1)
+        quantize_x(1, 0, 2)
+        product(1, 1)
         product(1, 0)
-        finish(1, False)
-        product(2, 1)
-        quantize_x(3, 1, 1)
-        finish(2, True)
+        quantize_x(3, 0, 2)
         product(3, 1)
+        product(0, 1)
+        finish(0, False)
+        product(2, 1)
+        finish(2, False)
+        product(3, 0)
+        finish(1, False)
         finish(3, False)

@@ -18,290 +18,261 @@ MULT = mybir.AluOpType.mult
 COPY = mybir.ActivationFunctionType.Copy
 
 P = 128
-PACK = 4
-K_PASS = P * PACK
-PASSES = T // K_PASS
-N_BLOCKS = DV // P
-D_BLOCKS = D // P
-LIST_COLS = K_PASS // 16
+SLOTS = 4
+HALF = P * SLOTS
+HALVES = T // HALF
+LIST_COLS = HALF // 16
+PSUM_BANKS = 8
+ALIGN = 64
+VECTOR_TILES = 25
+SCALAR_TILES = 16
 
 
 def tile_attend_gvq_cw_w_kernel(tc, zT, cb, tw, xT, offs, out):
     nc = tc.nc
     with ExitStack() as ctx:
         keep = ctx.enter_context(tc.tile_pool(name="keep", bufs=1))
-        psum = ctx.enter_context(tc.psum_pool(name="psum", bufs=8))
+        psum = ctx.enter_context(tc.psum_pool(name="psum", bufs=PSUM_BANKS))
+        vector_pool = ctx.enter_context(tc.tile_pool(name="by_vector", bufs=VECTOR_TILES))
+        scalar_pool = ctx.enter_context(tc.tile_pool(name="by_scalar", bufs=SCALAR_TILES))
 
-        by_vector = ctx.enter_context(tc.tile_pool(name="by_vector", bufs=26))
-        by_scalar = ctx.enter_context(tc.tile_pool(name="by_scalar", bufs=17))
+        def vector_tile(shape, dtype):
+            return vector_pool.tile(shape, dtype, name="made", tag="made", align_bytes=ALIGN)
 
-        def result_tile(on_vector, shape, dtype):
-            pool = by_vector if on_vector else by_scalar
-            return pool.tile(shape, dtype, name="made", tag="made", align_bytes=64)
+        def scalar_tile(shape, dtype):
+            return scalar_pool.tile(shape, dtype, name="made", tag="made", align_bytes=ALIGN)
+
+        def bank_tile(shape):
+            return psum.tile(shape, F32, name="bank", tag="bank")
+
+        on_vector = (vector_tile, nc.vector.tensor_copy)
+        on_scalar = (scalar_tile, nc.scalar.copy)
+
+        def rows(i):
+            return slice(i * P, (i + 1) * P)
 
         offsets = keep.tile([P, T // 16], U16, name="offsets")
-        cb_sb = [keep.tile([P, C], F32, name="cb%d" % b) for b in range(N_BLOCKS)]
-        z_sb = {}
-        x_sb = {}
-        whole = {}
+        codebook = {}
+        z_half = {}
+        x_half = {}
+        x_whole = {}
 
-        def load_cb(b):
-            nc.sync.dma_start(cb_sb[b][:], cb[b * P : (b + 1) * P, :])
+        def load_codebook(b):
+            codebook[b] = keep.tile([P, C], F32, name="cb%d" % b)
+            nc.sync.dma_start(codebook[b][:], cb[rows(b), :])
 
-        def load_rows(name, src, dst, b, g0, n):
-            rows = keep.tile([P, n * K_PASS], F32, name="%s%d_%d" % (name, b, g0))
-            nc.sync.dma_start(rows[:], src[b * P : (b + 1) * P, g0 * K_PASS : (g0 + n) * K_PASS])
-            whole[name, b] = rows
-            for g in range(n):
-                dst[b, g0 + g] = rows[:, g * K_PASS : (g + 1) * K_PASS]
+        def load_z(b):
+            whole = keep.tile([P, T], F32, name="z%d" % b)
+            nc.sync.dma_start(whole[:], zT[rows(b), :])
+            for h in range(HALVES):
+                z_half[b, h] = whole[:, h * HALF : (h + 1) * HALF]
 
-        def load_z(b, g0, n):
-            load_rows("z", zT, z_sb, b, g0, n)
+        def load_x(j):
+            x_whole[j] = keep.tile([P, T], F32, name="x%d" % j)
+            nc.sync.dma_start(x_whole[j][:], xT[rows(j), :])
+            for h in range(HALVES):
+                x_half[j, h] = x_whole[j][:, h * HALF : (h + 1) * HALF]
 
-        def load_x(j, g0, n):
-            load_rows("x", xT, x_sb, j, g0, n)
+        def load_x_half(j, h):
+            part = keep.tile([P, HALF], F32, name="x%d_%d" % (j, h))
+            nc.sync.dma_start(part[:], xT[rows(j), h * HALF : (h + 1) * HALF])
+            x_half[j, h] = part[:]
 
-        tw_sb = keep.tile([P, PASSES, 2 * PACK], F32, name="tw_sb")
-        nc.scalar.dma_start(tw_sb[:, :, 0:PACK], tw[0, :].rearrange("(g p t) -> p g t", g=PASSES, t=PACK))
+        tw_sb = keep.tile([P, HALVES, 2 * SLOTS], F32, name="tw_sb")
+        nc.scalar.dma_start(tw_sb[:, :, 0:SLOTS], tw[0, :].rearrange("(h p s) -> p h s", h=HALVES, s=SLOTS))
+
+        load_codebook(0)
         nc.sync.dma_start(offsets[:], offs)
-        load_cb(0)
-        load_z(0, 0, 2)
-        load_cb(1)
-        load_z(1, 0, 2)
-        load_cb(2)
-        load_z(2, 0, 2)
-        load_cb(3)
-        load_z(3, 0, 1)
-        load_z(3, 1, 1)
-        load_x(0, 0, 2)
-        load_x(1, 0, 2)
-        load_x(2, 0, 2)
-        load_x(3, 0, 1)
-        load_x(3, 1, 1)
+        for b in range(3):
+            load_z(b)
+            load_codebook(b + 1)
+        load_x(0)
+        load_z(3)
+        load_x(1)
+        load_x(2)
+        load_x_half(3, 0)
+        load_x_half(3, 1)
 
         ident = keep.tile([P, P], F32, name="ident")
         make_identity(nc, ident[:])
-        minus_one = keep.tile([P, K_PASS], F32, name="minus_one")
+        minus_one = keep.tile([P, HALF], F32, name="minus_one")
         nc.vector.memset(minus_one[:], -1.0)
-        scale = keep.tile([P, PASSES, PACK], F32, name="scale")
-        nc.scalar.activation(scale[:], tw_sb[:, :, 0:PACK], COPY, scale=BETA)
+        weight = keep.tile([P, HALVES, SLOTS], F32, name="weight")
+        nc.scalar.activation(weight[:], tw_sb[:, :, 0:SLOTS], COPY, scale=BETA)
 
-        g_bf = {}
-        g_codes = [keep.tile([P, DV], U32, name="g_codes%d" % g, align_bytes=64) for g in range(PASSES)]
-        g_scales = [keep.tile([P, DV], U8, name="g_scales%d" % g, align_bytes=64) for g in range(PASSES)]
-        neg_c = {}
-        g_pairs = {}
+        g_codes = [keep.tile([P, DV], U32, name="g_codes%d" % h, align_bytes=ALIGN) for h in range(HALVES)]
+        g_scales = [keep.tile([P, DV], U8, name="g_scales%d" % h, align_bytes=ALIGN) for h in range(HALVES)]
+        minus_c = {}
         e_bank = {}
+        g_pairs = {}
+        g_words = {}
+
+        def gather(b, h):
+            picked = vector_tile([P, HALF], F32)
+            listed = offsets[:, h * LIST_COLS : (h + 1) * LIST_COLS]
+            nc.vector.tensor_tensor(picked[:], codebook[b][:].indirect(listed), minus_one[:], MULT)
+            minus_c[b, h] = picked[:]
+
+        def add_turned(source, b, h):
+            first = (b, h) not in e_bank
+            if first:
+                e_bank[b, h] = bank_tile([P, SLOTS, P])
+            for s in range(SLOTS):
+                nc.tensor.matmul(
+                    e_bank[b, h][:, s, :],
+                    lhsT=source[b, h][:, s:HALF:SLOTS],
+                    rhs=ident[:],
+                    is_transpose=True,
+                    start=first and s == 0,
+                    stop=not first and s == SLOTS - 1,
+                )
+
+        def weigh_on_vector(b, h):
+            g_words[b, h] = vector_tile([P, P, SLOTS], BF16)
+            nc.vector.tensor_tensor(
+                g_words[b, h][:],
+                e_bank[b, h][:].rearrange("p s n -> p n s"),
+                weight[:, h, :].unsqueeze(1).to_broadcast([P, P, SLOTS]),
+                MULT,
+            )
+
+        def weigh_on_scalar(b, h):
+            pairs = scalar_tile([P, 2, P, 2], BF16)
+            for s in range(SLOTS):
+                nc.scalar.activation(
+                    pairs[:, s // 2, :, s % 2], e_bank[b, h][:, s, :], COPY, scale=weight[:, h, s : s + 1]
+                )
+            g_pairs[b, h] = pairs[:].rearrange("p u n e -> p (u n e)").bitcast(F32)
+
+        def join_pairs(b, h):
+            g_words[b, h] = vector_tile([P, P, SLOTS], BF16)
+            joined = g_words[b, h][:].rearrange("p n s -> p (n s)").bitcast(F32)
+            nc.vector.tensor_copy(
+                joined.rearrange("p (n u) -> p n u", u=2), g_pairs[b, h].rearrange("p (u n) -> p n u", u=2)
+            )
+
+        def quantize_g(b, h):
+            nc.vector.quantize_mx(
+                out=g_codes[h][:, rows(b)].bitcast(E5M2),
+                scales=g_scales[h][:, rows(b)],
+                in_=g_words[b, h][:].rearrange("p n s -> p (n s)"),
+            )
+
         x_pairs = {}
-        x_bf = {}
+        x_words = {}
         x_codes = {}
         x_scales = {}
-        acc = {}
 
-        def gather(b, g0, n):
-            picked = result_tile(True, [P, n * K_PASS], F32)
-            nc.vector.tensor_tensor(
-                picked[:],
-                cb_sb[b][:].indirect(offsets[:, g0 * LIST_COLS : (g0 + n) * LIST_COLS]),
-                minus_one[:, 0 : n * K_PASS],
-                MULT,
-            )
-            for g in range(n):
-                neg_c[b, g0 + g] = picked[:, g * K_PASS : (g + 1) * K_PASS]
-
-        def turn(src, b, g):
-            first = (b, g) not in e_bank
-            if first:
-                e_bank[b, g] = psum.tile([P, PACK, P], F32, name="bank", tag="bank")
-            for t in range(PACK):
-                nc.tensor.matmul(
-                    e_bank[b, g][:, t, :], lhsT=src[b, g][:, t:K_PASS:PACK], rhs=ident[:],
-                    is_transpose=True, start=(first and t == 0), stop=(not first and t == PACK - 1),
-                )
-
-        def weigh_vector(b, g):
-            g_bf[b, g] = result_tile(True, [P, P, PACK], BF16)
-            nc.vector.tensor_tensor(
-                g_bf[b, g][:],
-                e_bank[b, g][:].rearrange("p t n -> p n t"),
-                scale[:, g, :].unsqueeze(1).to_broadcast([P, P, PACK]),
-                MULT,
-            )
-
-        def weigh_act(b, g):
-            pairs = result_tile(False, [P, 2, P, 2], BF16)
-            for t in range(PACK):
-                nc.scalar.activation(
-                    pairs[:, t // 2, :, t % 2], e_bank[b, g][:, t, :], COPY, scale=scale[:, g, t : t + 1]
-                )
-            g_pairs[b, g] = pairs[:].rearrange("p u n e -> p (u n e)").bitcast(F32)
-
-        def interleave(b, g, n):
-            g_bf[b, g] = result_tile(True, [P, P, PACK], BF16)
-            dst = g_bf[b, g][:].rearrange("p n t -> p (n t)").bitcast(F32)
-            nc.vector.tensor_copy(
-                dst.rearrange("p (n u) -> p n u", u=2), g_pairs[b, g].rearrange("p (u n) -> p n u", u=2)
-            )
-
-        def quantize_g(g, b0, n):
-            cols = slice(b0 * P, (b0 + n) * P)
-            nc.vector.quantize_mx(
-                out=g_codes[g][:, cols].bitcast(E5M2),
-                scales=g_scales[g][:, cols],
-                in_=g_bf[b0, g][:].rearrange("p n t -> p (n t)"),
-            )
-
-        def cast_x(j, g, on_vector):
-            pairs = result_tile(on_vector, [P, 2, P, 2], BF16)
-            src = x_sb[j, g].rearrange("d (p u e) -> d u p e", u=2, e=2)
-            if on_vector:
-                nc.vector.tensor_copy(pairs[:], src)
-            else:
-                nc.scalar.copy(pairs[:], src)
-            words = pairs[:].rearrange("d u p e -> d (u p e)").bitcast(F32)
-            for u in range(2):
-                x_pairs[j, g, u] = words[:, u * P : (u + 1) * P]
-
-        def cast_both(j, on_vector):
-            pairs = result_tile(on_vector, [P, 2, PASSES * P, 2], BF16)
-            src = whole["x", j][:].rearrange("d (q u e) -> d u q e", u=2, e=2)
-            if on_vector:
-                nc.vector.tensor_copy(pairs[:], src)
-            else:
-                nc.scalar.copy(pairs[:], src)
+        def round_x(j, h0, halves, source, engine):
+            new_tile, copy = engine
+            pairs = new_tile([P, 2, halves * P, 2], BF16)
+            copy(pairs[:], source.rearrange("d (q u e) -> d u q e", u=2, e=2))
             words = pairs[:].rearrange("d u q e -> d (u q e)").bitcast(F32)
             for u in range(2):
-                for g in range(PASSES):
-                    x_pairs[j, g, u] = words[:, (u * PASSES + g) * P : (u * PASSES + g + 1) * P]
+                for h in range(halves):
+                    x_pairs[j, h0 + h, u] = words[:, rows(u * halves + h)]
 
-        def turn_x(j, g0, n, on_vector):
-            bank = psum.tile([P, n, 2, P], F32, name="bank", tag="bank")
-            for g in range(n):
+        def turn_x_pairs(j, h0, halves, engine):
+            new_tile, copy = engine
+            bank = bank_tile([P, halves, 2, P])
+            for h in range(halves):
                 for u in range(2):
-                    nc.tensor.transpose(bank[:, g, u, :], x_pairs[j, g0 + g, u], ident[:])
-            grouped = result_tile(on_vector, [P, n * P * PACK], BF16)
-            dst = grouped[:].bitcast(F32).rearrange("p (g d u) -> p g d u", g=n, u=2)
-            src = bank[:].rearrange("p g u d -> p g d u")
-            if on_vector:
-                nc.vector.tensor_copy(dst, src)
-            else:
-                nc.scalar.copy(dst, src)
-            x_bf[j, g0] = grouped
-
-        def turn_x32(j, g, on_vector):
-            bank = psum.tile([P, PACK, P], F32, name="bank", tag="bank")
-            for t in range(PACK):
-                nc.tensor.transpose(bank[:, t, :], x_sb[j, g][:, t:K_PASS:PACK], ident[:])
-            grouped = result_tile(on_vector, [P, P * PACK], BF16)
-            dst = grouped[:].rearrange("p (d t) -> p d t", t=PACK)
-            src = bank[:].rearrange("p t d -> p d t")
-            if on_vector:
-                nc.vector.tensor_copy(dst, src)
-            else:
-                nc.scalar.copy(dst, src)
-            x_bf[j, g] = grouped
-
-        def quantize_x(j, g0, n):
-            codes = result_tile(True, [P, n * P], U32)
-            scales = keep.tile([P, n * P], U8, name="x_scales%d_%d" % (j, g0), align_bytes=64)
-            nc.vector.quantize_mx(out=codes[:].bitcast(E4M3), scales=scales[:], in_=x_bf[j, g0][:])
-            for g in range(n):
-                x_codes[j, g0 + g] = codes[:, g * P : (g + 1) * P]
-                x_scales[j, g0 + g] = scales[:, g * P : (g + 1) * P]
-
-        def product(j, g):
-            first = j not in acc
-            if first:
-                acc[j] = psum.tile([P, DV], F32, name="bank", tag="bank")
-            nc.tensor.matmul_mx(
-                out=acc[j][:], lhsT=x_codes[j, g].bitcast(E4M3), lhsT_scale=x_scales[j, g],
-                rhs=g_codes[g][:].bitcast(E5M2), rhs_scale=g_scales[g][:],
-                start=first, stop=not first,
+                    nc.tensor.transpose(bank[:, h, u, :], x_pairs[j, h0 + h, u], ident[:])
+            x_words[j, h0] = new_tile([P, halves * HALF], BF16)
+            copy(
+                x_words[j, h0][:].bitcast(F32).rearrange("p (h d u) -> p h d u", h=halves, u=2),
+                bank[:].rearrange("p h u d -> p h d u"),
             )
 
-        def finish(j, on_vector, parts=1):
-            width = DV // parts
-            for h in range(parts):
-                cols = slice(h * width, (h + 1) * width)
-                result = result_tile(on_vector, [P, width], F32)
-                if on_vector:
-                    nc.vector.tensor_copy(result[:], acc[j][:, cols])
-                else:
-                    nc.scalar.copy(result[:], acc[j][:, cols])
-                nc.sync.dma_start(out[j * P : (j + 1) * P, cols], result[:])
+        def turn_x_float32(j, h):
+            bank = bank_tile([P, SLOTS, P])
+            for s in range(SLOTS):
+                nc.tensor.transpose(bank[:, s, :], x_half[j, h][:, s:HALF:SLOTS], ident[:])
+            x_words[j, h] = scalar_tile([P, HALF], BF16)
+            nc.scalar.copy(
+                x_words[j, h][:].rearrange("p (d s) -> p d s", s=SLOTS), bank[:].rearrange("p s d -> p d s")
+            )
 
-        gather(0, 0, 1)
-        turn(z_sb, 0, 0)
-        turn(neg_c, 0, 0)
-        gather(0, 1, 1)
-        turn(z_sb, 0, 1)
-        turn(neg_c, 0, 1)
-        weigh_act(0, 0)
-        weigh_act(0, 1)
-        gather(1, 0, 1)
-        interleave(0, 0, 1)
-        turn(z_sb, 1, 0)
-        turn(neg_c, 1, 0)
-        gather(1, 1, 1)
-        interleave(0, 1, 1)
-        turn(z_sb, 1, 1)
-        turn(neg_c, 1, 1)
-        quantize_g(0, 0, 1)
-        quantize_g(1, 0, 1)
-        weigh_act(1, 0)
-        weigh_act(1, 1)
-        gather(2, 0, 1)
-        interleave(1, 0, 1)
-        turn(z_sb, 2, 0)
-        turn(neg_c, 2, 0)
-        gather(2, 1, 1)
-        interleave(1, 1, 1)
-        turn(z_sb, 2, 1)
-        turn(neg_c, 2, 1)
-        quantize_g(0, 1, 1)
-        quantize_g(1, 1, 1)
-        weigh_act(2, 0)
-        weigh_act(2, 1)
-        gather(3, 0, 1)
-        interleave(2, 0, 1)
-        turn(z_sb, 3, 0)
-        turn(neg_c, 3, 0)
-        gather(3, 1, 1)
-        interleave(2, 1, 1)
-        turn(z_sb, 3, 1)
-        turn(neg_c, 3, 1)
-        cast_both(0, False)
-        weigh_vector(3, 0)
-        cast_both(1, False)
-        turn_x(0, 0, 1, True)
-        turn_x(0, 1, 1, True)
+        def quantize_x(j, h0, halves):
+            codes = vector_tile([P, halves * P], U32)
+            scales = keep.tile([P, halves * P], U8, name="x_scales%d_%d" % (j, h0), align_bytes=ALIGN)
+            nc.vector.quantize_mx(out=codes[:].bitcast(E4M3), scales=scales[:], in_=x_words[j, h0][:])
+            for h in range(halves):
+                x_codes[j, h0 + h] = codes[:, rows(h)]
+                x_scales[j, h0 + h] = scales[:, rows(h)]
+
+        sums = {}
+
+        def product(j, h):
+            if h == 0:
+                sums[j] = bank_tile([P, DV])
+            nc.tensor.matmul_mx(
+                out=sums[j][:],
+                lhsT=x_codes[j, h].bitcast(E4M3),
+                lhsT_scale=x_scales[j, h],
+                rhs=g_codes[h][:].bitcast(E5M2),
+                rhs_scale=g_scales[h][:],
+                start=h == 0,
+                stop=h == HALVES - 1,
+            )
+
+        def store(j, engine):
+            new_tile, copy = engine
+            result = new_tile([P, DV], F32)
+            copy(result[:], sums[j][:])
+            nc.sync.dma_start(out[rows(j), :], result[:])
+
+        for b in range(3):
+            for h in range(HALVES):
+                gather(b, h)
+                if b > 0:
+                    join_pairs(b - 1, h)
+                add_turned(z_half, b, h)
+                add_turned(minus_c, b, h)
+            if b > 0:
+                for h in range(HALVES):
+                    quantize_g(b - 1, h)
+            for h in range(HALVES):
+                weigh_on_scalar(b, h)
+
+        gather(3, 0)
+        join_pairs(2, 0)
+        turn_x_float32(0, 0)
+        turn_x_float32(0, 1)
+        add_turned(minus_c, 3, 0)
+        gather(3, 1)
         quantize_x(0, 0, 1)
-        cast_both(2, False)
-        cast_x(3, 0, True)
-        weigh_vector(3, 1)
-        quantize_g(0, 2, 1)
-        cast_x(3, 1, False)
-        quantize_g(0, 3, 1)
-        turn_x(1, 0, 2, False)
+        add_turned(z_half, 3, 0)
+        weigh_on_vector(3, 0)
+        round_x(1, 0, HALVES, x_whole[1][:], on_scalar)
+        quantize_g(2, 0)
+        round_x(2, 0, HALVES, x_whole[2][:], on_scalar)
+        round_x(3, 0, 1, x_half[3, 0], on_vector)
+        join_pairs(2, 1)
+        add_turned(minus_c, 3, 1)
+        quantize_g(3, 0)
+        turn_x_pairs(1, 0, HALVES, on_scalar)
+        add_turned(z_half, 3, 1)
+        weigh_on_vector(3, 1)
+        quantize_g(2, 1)
         quantize_x(0, 1, 1)
         product(0, 0)
-        turn_x(2, 1, 1, False)
-        quantize_g(1, 3, 1)
-        turn_x(2, 0, 1, True)
-        turn_x(3, 0, 2, False)
-        quantize_x(2, 0, 1)
-        quantize_x(2, 1, 1)
-        product(2, 0)
-        quantize_g(1, 2, 1)
-        quantize_x(1, 0, 2)
-        product(1, 1)
-        product(1, 0)
-        quantize_x(3, 0, 2)
-        product(3, 1)
+        quantize_g(3, 1)
+        turn_x_pairs(2, 0, HALVES, on_scalar)
+        turn_x_float32(3, 1)
+        quantize_x(1, 0, HALVES)
+        turn_x_pairs(3, 0, 1, on_vector)
         product(0, 1)
-        finish(0, False)
+        store(0, on_scalar)
+        product(1, 0)
+        quantize_x(2, 0, HALVES)
+        product(1, 1)
+        quantize_x(3, 1, 1)
+        product(2, 0)
         product(2, 1)
-        finish(2, False)
+        quantize_x(3, 0, 1)
+        store(1, on_scalar)
         product(3, 0)
-        finish(1, False)
-        finish(3, False)
+        product(3, 1)
+        store(2, on_vector)
+        store(3, on_scalar)

@@ -22,10 +22,11 @@ SLOTS = 4
 HALF = P * SLOTS
 HALVES = T // HALF
 LIST_COLS = HALF // 16
+LAST = 3
 PSUM_BANKS = 8
 ALIGN = 64
-VECTOR_TILES = 25
-SCALAR_TILES = 16
+VECTOR_TILES = 24
+SCALAR_TILES = 15
 
 
 def tile_attend_gvq_cw_w_kernel(tc, zT, cb, tw, xT, offs, out):
@@ -61,37 +62,31 @@ def tile_attend_gvq_cw_w_kernel(tc, zT, cb, tw, xT, offs, out):
             codebook[b] = keep.tile([P, C], F32, name="cb%d" % b)
             nc.sync.dma_start(codebook[b][:], cb[rows(b), :])
 
-        def load_z(b):
-            whole = keep.tile([P, T], F32, name="z%d" % b)
-            nc.sync.dma_start(whole[:], zT[rows(b), :])
+        def load_whole(source, name, i, halves):
+            whole = keep.tile([P, T], F32, name="%s%d" % (name, i))
+            nc.sync.dma_start(whole[:], source[rows(i), :])
             for h in range(HALVES):
-                z_half[b, h] = whole[:, h * HALF : (h + 1) * HALF]
+                halves[i, h] = whole[:, h * HALF : (h + 1) * HALF]
+            return whole
 
-        def load_x(j):
-            x_whole[j] = keep.tile([P, T], F32, name="x%d" % j)
-            nc.sync.dma_start(x_whole[j][:], xT[rows(j), :])
+        def load_by_halves(source, name, i, halves):
             for h in range(HALVES):
-                x_half[j, h] = x_whole[j][:, h * HALF : (h + 1) * HALF]
-
-        def load_x_half(j, h):
-            part = keep.tile([P, HALF], F32, name="x%d_%d" % (j, h))
-            nc.sync.dma_start(part[:], xT[rows(j), h * HALF : (h + 1) * HALF])
-            x_half[j, h] = part[:]
+                part = keep.tile([P, HALF], F32, name="%s%d_%d" % (name, i, h))
+                nc.sync.dma_start(part[:], source[rows(i), h * HALF : (h + 1) * HALF])
+                halves[i, h] = part[:]
 
         tw_sb = keep.tile([P, HALVES, 2 * SLOTS], F32, name="tw_sb")
         nc.scalar.dma_start(tw_sb[:, :, 0:SLOTS], tw[0, :].rearrange("(h p s) -> p h s", h=HALVES, s=SLOTS))
 
         load_codebook(0)
         nc.sync.dma_start(offsets[:], offs)
-        for b in range(3):
-            load_z(b)
+        for b in range(LAST):
+            load_whole(zT, "z", b, z_half)
             load_codebook(b + 1)
-        load_x(0)
-        load_z(3)
-        load_x(1)
-        load_x(2)
-        load_x_half(3, 0)
-        load_x_half(3, 1)
+        load_by_halves(zT, "z", LAST, z_half)
+        for j in range(LAST):
+            x_whole[j] = load_whole(xT, "x", j, x_half)
+        load_by_halves(xT, "x", LAST, x_half)
 
         ident = keep.tile([P, P], F32, name="ident")
         make_identity(nc, ident[:])
@@ -99,6 +94,15 @@ def tile_attend_gvq_cw_w_kernel(tc, zT, cb, tw, xT, offs, out):
         nc.vector.memset(minus_one[:], -1.0)
         weight = keep.tile([P, HALVES, SLOTS], F32, name="weight")
         nc.scalar.activation(weight[:], tw_sb[:, :, 0:SLOTS], COPY, scale=BETA)
+
+        ones = keep.tile([P, DV * SLOTS], BF16, name="ones", align_bytes=ALIGN)
+        nc.vector.memset(ones[:], 1.0)
+        warm_moving = keep.tile([P, DV], U32, name="warm_moving", align_bytes=ALIGN)
+        warm_moving_scales = keep.tile([P, DV], U8, name="warm_moving_scales", align_bytes=ALIGN)
+        nc.vector.quantize_mx(out=warm_moving[:].bitcast(E5M2), scales=warm_moving_scales[:], in_=ones[:])
+        warm_fixed = keep.tile([P, P], U32, name="warm_fixed", align_bytes=ALIGN)
+        warm_fixed_scales = keep.tile([P, P], U8, name="warm_fixed_scales", align_bytes=ALIGN)
+        nc.vector.quantize_mx(out=warm_fixed[:].bitcast(E4M3), scales=warm_fixed_scales[:], in_=ones[:, 0:HALF])
 
         g_codes = [keep.tile([P, DV], U32, name="g_codes%d" % h, align_bytes=ALIGN) for h in range(HALVES)]
         g_scales = [keep.tile([P, DV], U8, name="g_scales%d" % h, align_bytes=ALIGN) for h in range(HALVES)]
@@ -184,15 +188,6 @@ def tile_attend_gvq_cw_w_kernel(tc, zT, cb, tw, xT, offs, out):
                 bank[:].rearrange("p h u d -> p h d u"),
             )
 
-        def turn_x_float32(j, h):
-            bank = bank_tile([P, SLOTS, P])
-            for s in range(SLOTS):
-                nc.tensor.transpose(bank[:, s, :], x_half[j, h][:, s:HALF:SLOTS], ident[:])
-            x_words[j, h] = scalar_tile([P, HALF], BF16)
-            nc.scalar.copy(
-                x_words[j, h][:].rearrange("p (d s) -> p d s", s=SLOTS), bank[:].rearrange("p s d -> p d s")
-            )
-
         def quantize_x(j, h0, halves):
             codes = vector_tile([P, halves * P], U32)
             scales = keep.tile([P, halves * P], U8, name="x_scales%d_%d" % (j, h0), align_bytes=ALIGN)
@@ -216,13 +211,24 @@ def tile_attend_gvq_cw_w_kernel(tc, zT, cb, tw, xT, offs, out):
                 stop=h == HALVES - 1,
             )
 
+        def warm_up():
+            nc.tensor.matmul_mx(
+                out=bank_tile([P, DV])[:],
+                lhsT=warm_fixed[:].bitcast(E4M3),
+                lhsT_scale=warm_fixed_scales[:],
+                rhs=warm_moving[:].bitcast(E5M2),
+                rhs_scale=warm_moving_scales[:],
+                start=True,
+                stop=True,
+            )
+
         def store(j, engine):
             new_tile, copy = engine
             result = new_tile([P, DV], F32)
             copy(result[:], sums[j][:])
             nc.sync.dma_start(out[rows(j), :], result[:])
 
-        for b in range(3):
+        for b in range(LAST):
             for h in range(HALVES):
                 gather(b, h)
                 if b > 0:
@@ -236,43 +242,43 @@ def tile_attend_gvq_cw_w_kernel(tc, zT, cb, tw, xT, offs, out):
                 weigh_on_scalar(b, h)
 
         gather(3, 0)
-        join_pairs(2, 0)
-        turn_x_float32(0, 0)
-        turn_x_float32(0, 1)
-        add_turned(minus_c, 3, 0)
-        gather(3, 1)
-        quantize_x(0, 0, 1)
+        round_x(0, 0, HALVES, x_whole[0][:], on_scalar)
         add_turned(z_half, 3, 0)
-        weigh_on_vector(3, 0)
+        gather(3, 1)
         round_x(1, 0, HALVES, x_whole[1][:], on_scalar)
-        quantize_g(2, 0)
-        round_x(2, 0, HALVES, x_whole[2][:], on_scalar)
-        round_x(3, 0, 1, x_half[3, 0], on_vector)
+        add_turned(minus_c, 3, 0)
+        add_turned(z_half, 3, 1)
+        join_pairs(2, 0)
         join_pairs(2, 1)
         add_turned(minus_c, 3, 1)
-        quantize_g(3, 0)
-        turn_x_pairs(1, 0, HALVES, on_scalar)
-        add_turned(z_half, 3, 1)
-        weigh_on_vector(3, 1)
+        turn_x_pairs(0, 0, HALVES, on_scalar)
+        warm_up()
+        warm_up()
+        weigh_on_vector(3, 0)
+        quantize_g(2, 0)
         quantize_g(2, 1)
-        quantize_x(0, 1, 1)
-        product(0, 0)
+        quantize_g(3, 0)
+        round_x(2, 0, HALVES, x_whole[2][:], on_vector)
+        weigh_on_vector(3, 1)
+        round_x(3, 0, 1, x_half[3, 0], on_scalar)
+        round_x(3, 1, 1, x_half[3, 1], on_vector)
+        quantize_x(0, 0, HALVES)
+        turn_x_pairs(1, 0, HALVES, on_scalar)
         quantize_g(3, 1)
         turn_x_pairs(2, 0, HALVES, on_scalar)
-        turn_x_float32(3, 1)
-        quantize_x(1, 0, HALVES)
-        turn_x_pairs(3, 0, 1, on_vector)
+        turn_x_pairs(3, 0, HALVES, on_scalar)
+        product(0, 0)
         product(0, 1)
-        store(0, on_scalar)
-        product(1, 0)
+        quantize_x(1, 0, HALVES)
         quantize_x(2, 0, HALVES)
+        quantize_x(3, 0, HALVES)
+        product(1, 0)
         product(1, 1)
-        quantize_x(3, 1, 1)
+        store(0, on_scalar)
         product(2, 0)
         product(2, 1)
-        quantize_x(3, 0, 1)
-        store(1, on_scalar)
         product(3, 0)
         product(3, 1)
-        store(2, on_vector)
-        store(3, on_scalar)
+        store(1, on_vector)
+        store(2, on_scalar)
+        store(3, on_vector)

@@ -15,6 +15,8 @@ U8 = mybir.dt.uint8
 E4M3 = mybir.dt.float8_e4m3fn_x4
 E5M2 = mybir.dt.float8_e5m2_x4
 MULT = mybir.AluOpType.mult
+SUBTRACT = mybir.AluOpType.subtract
+ADD = mybir.AluOpType.add
 COPY = mybir.ActivationFunctionType.Copy
 
 P = 128
@@ -25,8 +27,8 @@ LIST_COLS = HALF // 16
 LAST = 3
 PSUM_BANKS = 8
 ALIGN = 64
-VECTOR_TILES = 24
-SCALAR_TILES = 15
+VECTOR_TILES = 32
+SCALAR_TILES = 24
 
 
 def tile_attend_gvq_cw_w_kernel(tc, zT, cb, tw, xT, offs, out):
@@ -62,38 +64,43 @@ def tile_attend_gvq_cw_w_kernel(tc, zT, cb, tw, xT, offs, out):
             codebook[b] = keep.tile([P, C], F32, name="cb%d" % b)
             nc.sync.dma_start(codebook[b][:], cb[rows(b), :])
 
-        def load_whole(source, name, i, halves):
+        sources = {"z": (zT, z_half), "x": (xT, x_half)}
+
+        def load_offsets():
+            nc.sync.dma_start(offsets[:], offs)
+
+        def load_whole(name, i):
+            source, halves = sources[name]
             whole = keep.tile([P, T], F32, name="%s%d" % (name, i))
             nc.sync.dma_start(whole[:], source[rows(i), :])
             for h in range(HALVES):
                 halves[i, h] = whole[:, h * HALF : (h + 1) * HALF]
-            return whole
+            if name == "x":
+                x_whole[i] = whole[:]
 
-        def load_by_halves(source, name, i, halves):
-            for h in range(HALVES):
-                part = keep.tile([P, HALF], F32, name="%s%d_%d" % (name, i, h))
-                nc.sync.dma_start(part[:], source[rows(i), h * HALF : (h + 1) * HALF])
-                halves[i, h] = part[:]
+        def load_half(name, i, h):
+            source, halves = sources[name]
+            part = keep.tile([P, HALF], F32, name="%s%d_%d" % (name, i, h))
+            nc.sync.dma_start(part[:], source[rows(i), h * HALF : (h + 1) * HALF])
+            halves[i, h] = part[:]
 
         tw_sb = keep.tile([P, HALVES, 2 * SLOTS], F32, name="tw_sb")
         nc.scalar.dma_start(tw_sb[:, :, 0:SLOTS], tw[0, :].rearrange("(h p s) -> p h s", h=HALVES, s=SLOTS))
 
         load_codebook(0)
-        nc.sync.dma_start(offsets[:], offs)
-        for b in range(LAST):
-            load_whole(zT, "z", b, z_half)
-            load_codebook(b + 1)
-        load_by_halves(zT, "z", LAST, z_half)
-        for j in range(LAST):
-            x_whole[j] = load_whole(xT, "x", j, x_half)
-        load_by_halves(xT, "x", LAST, x_half)
+        load_offsets()
+        load_whole('z',0); load_codebook(1); load_whole('z',1); load_codebook(2); load_whole('z',2)
+        load_whole('x',0)
+        load_codebook(3)
+        load_half('z',3,0); load_half('z',3,1)
+        load_whole('x',1);load_whole('x',2)
+        load_half('x',3,0); load_half('x',3,1)
 
         ident = keep.tile([P, P], F32, name="ident")
         make_identity(nc, ident[:])
-        minus_one = keep.tile([P, HALF], F32, name="minus_one")
-        nc.vector.memset(minus_one[:], -1.0)
         weight = keep.tile([P, HALVES, SLOTS], F32, name="weight")
-        nc.scalar.activation(weight[:], tw_sb[:, :, 0:SLOTS], COPY, scale=BETA)
+        nc.scalar.activation(weight[:, 0, :], tw_sb[:, 0, 0:SLOTS], COPY, scale=BETA)
+        nc.scalar.activation(weight[:, 1, :], tw_sb[:, 1, 0:SLOTS], COPY, scale=-BETA)
 
         ones = keep.tile([P, DV * SLOTS], BF16, name="ones", align_bytes=ALIGN)
         nc.vector.memset(ones[:], 1.0)
@@ -106,18 +113,37 @@ def tile_attend_gvq_cw_w_kernel(tc, zT, cb, tw, xT, offs, out):
 
         g_codes = [keep.tile([P, DV], U32, name="g_codes%d" % h, align_bytes=ALIGN) for h in range(HALVES)]
         g_scales = [keep.tile([P, DV], U8, name="g_scales%d" % h, align_bytes=ALIGN) for h in range(HALVES)]
-        minus_c = {}
+        minus_e = {}
         e_bank = {}
         g_pairs = {}
         g_words = {}
 
+        weight_rows = {}
+        g_turned = {}
+
+        def spread_weights(h):
+            spread = keep.tile([P, SLOTS, P], F32, name="spread%d" % h)
+            nc.scalar.copy(spread[:], weight[:, h, :].unsqueeze(2).to_broadcast([P, SLOTS, P]))
+            bank = bank_tile([P, SLOTS, P])
+            for s in range(SLOTS):
+                nc.tensor.transpose(bank[:, s, :], spread[:, s, :], ident[:])
+            weight_rows[h] = scalar_tile([P, 2, P, 2], F32)
+            nc.scalar.copy(weight_rows[h][:], bank[:].rearrange("q (u e) p -> q u p e", u=2))
+
         def gather(b, h):
             picked = vector_tile([P, HALF], F32)
             listed = offsets[:, h * LIST_COLS : (h + 1) * LIST_COLS]
-            nc.vector.tensor_tensor(picked[:], codebook[b][:].indirect(listed), minus_one[:], MULT)
-            minus_c[b, h] = picked[:]
+            nc.vector.tensor_tensor(picked[:], codebook[b][:].indirect(listed), z_half[b, h], SUBTRACT)
+            minus_e[b, h] = picked[:]
 
-        def add_turned(source, b, h):
+        def gather_minus(b, h):
+            picked = vector_tile([P, HALF], F32)
+            listed = offsets[:, h * LIST_COLS : (h + 1) * LIST_COLS]
+            nc.vector.tensor_scalar(picked[:], codebook[b][:].indirect(listed), -1.0, 0.0, MULT, ADD)
+            minus_e[b, h] = picked[:]
+
+        def add_turned(name, b, h):
+            source = z_half if name == "z" else minus_e
             first = (b, h) not in e_bank
             if first:
                 e_bank[b, h] = bank_tile([P, SLOTS, P])
@@ -130,6 +156,31 @@ def tile_attend_gvq_cw_w_kernel(tc, zT, cb, tw, xT, offs, out):
                     start=first and s == 0,
                     stop=not first and s == SLOTS - 1,
                 )
+
+        def turn_e(b, h):
+            e_bank[b, h] = bank_tile([P, SLOTS, P])
+            for s in range(SLOTS):
+                nc.tensor.transpose(e_bank[b, h][:, s, :], minus_e[b, h][:, s:HALF:SLOTS], ident[:])
+
+        def weigh_rows(b, h):
+            pairs = vector_tile([P, 2, P, 2], BF16)
+            nc.vector.tensor_tensor(
+                pairs[:], minus_e[b, h].rearrange("n (p u e) -> n u p e", u=2, e=2), weight_rows[h][:], MULT
+            )
+            g_pairs[b, h] = pairs[:].rearrange("n u p e -> n (u p e)").bitcast(F32)
+
+        def turn_g_pairs(b, h):
+            g_turned[b, h] = bank_tile([P, 2, P])
+            for u in range(2):
+                nc.tensor.transpose(g_turned[b, h][:, u, :], g_pairs[b, h][:, rows(u)], ident[:])
+
+        def join_turned_g(b, h, engine):
+            new_tile, copy = engine
+            g_words[b, h] = new_tile([P, P, SLOTS], BF16)
+            copy(
+                g_words[b, h][:].rearrange("p n s -> p (n s)").bitcast(F32).rearrange("p (n u) -> p n u", u=2),
+                g_turned[b, h][:].rearrange("p u n -> p n u"),
+            )
 
         def weigh_on_vector(b, h):
             g_words[b, h] = vector_tile([P, P, SLOTS], BF16)
@@ -148,10 +199,11 @@ def tile_attend_gvq_cw_w_kernel(tc, zT, cb, tw, xT, offs, out):
                 )
             g_pairs[b, h] = pairs[:].rearrange("p u n e -> p (u n e)").bitcast(F32)
 
-        def join_pairs(b, h):
-            g_words[b, h] = vector_tile([P, P, SLOTS], BF16)
+        def join_pairs(b, h, engine):
+            new_tile, copy = engine
+            g_words[b, h] = new_tile([P, P, SLOTS], BF16)
             joined = g_words[b, h][:].rearrange("p n s -> p (n s)").bitcast(F32)
-            nc.vector.tensor_copy(
+            copy(
                 joined.rearrange("p (n u) -> p n u", u=2), g_pairs[b, h].rearrange("p (u n) -> p n u", u=2)
             )
 
@@ -167,8 +219,9 @@ def tile_attend_gvq_cw_w_kernel(tc, zT, cb, tw, xT, offs, out):
         x_codes = {}
         x_scales = {}
 
-        def round_x(j, h0, halves, source, engine):
+        def round_x(j, h0, halves, engine):
             new_tile, copy = engine
+            source = x_whole[j] if halves == HALVES else x_half[j, h0]
             pairs = new_tile([P, 2, halves * P, 2], BF16)
             copy(pairs[:], source.rearrange("d (q u e) -> d u q e", u=2, e=2))
             words = pairs[:].rearrange("d u q e -> d (u q e)").bitcast(F32)
@@ -176,12 +229,18 @@ def tile_attend_gvq_cw_w_kernel(tc, zT, cb, tw, xT, offs, out):
                 for h in range(halves):
                     x_pairs[j, h0 + h, u] = words[:, rows(u * halves + h)]
 
-        def turn_x_pairs(j, h0, halves, engine):
-            new_tile, copy = engine
+        x_turned = {}
+
+        def turn_x(j, h0, halves):
             bank = bank_tile([P, halves, 2, P])
+            x_turned[j, h0] = bank
             for h in range(halves):
                 for u in range(2):
                     nc.tensor.transpose(bank[:, h, u, :], x_pairs[j, h0 + h, u], ident[:])
+
+        def join_x(j, h0, halves, engine):
+            new_tile, copy = engine
+            bank = x_turned[j, h0]
             x_words[j, h0] = new_tile([P, halves * HALF], BF16)
             copy(
                 x_words[j, h0][:].bitcast(F32).rearrange("p (h d u) -> p h d u", h=halves, u=2),
@@ -199,7 +258,8 @@ def tile_attend_gvq_cw_w_kernel(tc, zT, cb, tw, xT, offs, out):
         sums = {}
 
         def product(j, h):
-            if h == 0:
+            first = j not in sums
+            if first:
                 sums[j] = bank_tile([P, DV])
             nc.tensor.matmul_mx(
                 out=sums[j][:],
@@ -207,8 +267,8 @@ def tile_attend_gvq_cw_w_kernel(tc, zT, cb, tw, xT, offs, out):
                 lhsT_scale=x_scales[j, h],
                 rhs=g_codes[h][:].bitcast(E5M2),
                 rhs_scale=g_scales[h][:],
-                start=h == 0,
-                stop=h == HALVES - 1,
+                start=first,
+                stop=not first,
             )
 
         def warm_up():
@@ -222,63 +282,82 @@ def tile_attend_gvq_cw_w_kernel(tc, zT, cb, tw, xT, offs, out):
                 stop=True,
             )
 
-        def store(j, engine):
+        def store(j, engine, parts=1):
             new_tile, copy = engine
-            result = new_tile([P, DV], F32)
-            copy(result[:], sums[j][:])
-            nc.sync.dma_start(out[rows(j), :], result[:])
+            width = DV // parts
+            for k in range(parts):
+                result = new_tile([P, width], F32)
+                copy(result[:], sums[j][:, k * width : (k + 1) * width])
+                nc.sync.dma_start(out[rows(j), k * width : (k + 1) * width], result[:])
 
-        for b in range(LAST):
-            for h in range(HALVES):
-                gather(b, h)
+        for b in range(2):
+            gather_minus(b, 0)
+            add_turned('z', b, 0)
+            add_turned('d', b, 0)
+            gather(b, 1)
+            turn_e(b, 1)
+            for h in range(2):
+                weigh_on_scalar(b, h)
                 if b > 0:
-                    join_pairs(b - 1, h)
-                add_turned(z_half, b, h)
-                add_turned(minus_c, b, h)
+                    join_pairs(0, h, on_vector)
             if b > 0:
                 for h in range(HALVES):
-                    quantize_g(b - 1, h)
-            for h in range(HALVES):
-                weigh_on_scalar(b, h)
-
-        gather(3, 0)
-        round_x(0, 0, HALVES, x_whole[0][:], on_scalar)
-        add_turned(z_half, 3, 0)
+                    quantize_g(0, h)
+            if b == 0:
+                spread_weights(1)
+        gather_minus(2, 0)
+        add_turned('z', 2, 0)
+        add_turned('d', 2, 0)
+        gather(2, 1)
+        round_x(0,0,2,on_scalar)
+        join_pairs(1,0,on_vector)
+        weigh_rows(2,1)
+        turn_g_pairs(2,1)
+        turn_x(0,0,2)
+        join_pairs(1,1,on_vector)
+        quantize_g(1,0)
+        quantize_g(1,1)
+        weigh_on_scalar(2,0)
+        join_turned_g(2,1,on_vector)
+        gather_minus(3, 0)
+        add_turned('z', 3, 0)
+        add_turned('d', 3, 0)
+        join_x(0,0,2,on_scalar)
         gather(3, 1)
-        round_x(1, 0, HALVES, x_whole[1][:], on_scalar)
-        add_turned(minus_c, 3, 0)
-        add_turned(z_half, 3, 1)
-        join_pairs(2, 0)
-        join_pairs(2, 1)
-        add_turned(minus_c, 3, 1)
-        turn_x_pairs(0, 0, HALVES, on_scalar)
         warm_up()
         warm_up()
-        weigh_on_vector(3, 0)
-        quantize_g(2, 0)
+        round_x(1, 0, HALVES, on_scalar)
+        join_pairs(2,0,on_vector)
         quantize_g(2, 1)
-        quantize_g(3, 0)
-        round_x(2, 0, HALVES, x_whole[2][:], on_vector)
-        weigh_on_vector(3, 1)
-        round_x(3, 0, 1, x_half[3, 0], on_scalar)
-        round_x(3, 1, 1, x_half[3, 1], on_vector)
+        weigh_rows(3,1)
+        turn_g_pairs(3,1)
+        turn_x(1,0,2)
+        weigh_on_vector(3,0)
+        round_x(2, 0, HALVES, on_scalar)
+        turn_x(2,0,2)
+        quantize_g(2, 0)
         quantize_x(0, 0, HALVES)
-        turn_x_pairs(1, 0, HALVES, on_scalar)
+        quantize_g(3, 0)
+        join_turned_g(3,1,on_vector)
+        round_x(3, 0, 1, on_vector)
         quantize_g(3, 1)
-        turn_x_pairs(2, 0, HALVES, on_scalar)
-        turn_x_pairs(3, 0, HALVES, on_scalar)
+        round_x(3, 1, 1, on_vector)
         product(0, 0)
         product(0, 1)
+        turn_x(3,0,2)
+        join_x(1,0,2,on_scalar)
+        join_x(2,0,2,on_scalar)
         quantize_x(1, 0, HALVES)
-        quantize_x(2, 0, HALVES)
-        quantize_x(3, 0, HALVES)
         product(1, 0)
         product(1, 1)
-        store(0, on_scalar)
+        store(0, on_vector)
+        join_x(3,0,2,on_scalar)
+        quantize_x(2, 0, HALVES)
         product(2, 0)
         product(2, 1)
+        quantize_x(3, 0, HALVES)
+        store(1, on_scalar)
         product(3, 0)
         product(3, 1)
-        store(1, on_vector)
-        store(2, on_scalar)
-        store(3, on_vector)
+        store(2, on_vector)
+        store(3, on_scalar)

@@ -90,9 +90,9 @@ def tile_attend_gvq_cw_w_kernel(tc, zT, cb, tw, xT, offs, out):
         load_codebook(0)
         load_offsets()
         load_whole('z',0); load_codebook(1); load_whole('z',1); load_codebook(2); load_whole('z',2)
-        load_whole('x',0)
         load_codebook(3)
         load_half('z',3,0); load_half('z',3,1)
+        load_whole('x',0)
         load_whole('x',1);load_whole('x',2)
         load_half('x',3,0); load_half('x',3,1)
 
@@ -111,24 +111,12 @@ def tile_attend_gvq_cw_w_kernel(tc, zT, cb, tw, xT, offs, out):
         warm_fixed_scales = keep.tile([P, P], U8, name="warm_fixed_scales", align_bytes=ALIGN)
         nc.vector.quantize_mx(out=warm_fixed[:].bitcast(E4M3), scales=warm_fixed_scales[:], in_=ones[:, 0:HALF])
 
-        g_codes = [keep.tile([P, DV], U32, name="g_codes%d" % h, align_bytes=ALIGN) for h in range(HALVES)]
+        g_codes = {}
         g_scales = [keep.tile([P, DV], U8, name="g_scales%d" % h, align_bytes=ALIGN) for h in range(HALVES)]
         minus_e = {}
         e_bank = {}
         g_pairs = {}
         g_words = {}
-
-        weight_rows = {}
-        g_turned = {}
-
-        def spread_weights(h):
-            spread = keep.tile([P, SLOTS, P], F32, name="spread%d" % h)
-            nc.scalar.copy(spread[:], weight[:, h, :].unsqueeze(2).to_broadcast([P, SLOTS, P]))
-            bank = bank_tile([P, SLOTS, P])
-            for s in range(SLOTS):
-                nc.tensor.transpose(bank[:, s, :], spread[:, s, :], ident[:])
-            weight_rows[h] = scalar_tile([P, 2, P, 2], F32)
-            nc.scalar.copy(weight_rows[h][:], bank[:].rearrange("q (u e) p -> q u p e", u=2))
 
         def gather(b, h):
             picked = vector_tile([P, HALF], F32)
@@ -162,30 +150,14 @@ def tile_attend_gvq_cw_w_kernel(tc, zT, cb, tw, xT, offs, out):
             for s in range(SLOTS):
                 nc.tensor.transpose(e_bank[b, h][:, s, :], minus_e[b, h][:, s:HALF:SLOTS], ident[:])
 
-        def weigh_rows(b, h):
-            pairs = vector_tile([P, 2, P, 2], BF16)
-            nc.vector.tensor_tensor(
-                pairs[:], minus_e[b, h].rearrange("n (p u e) -> n u p e", u=2, e=2), weight_rows[h][:], MULT
-            )
-            g_pairs[b, h] = pairs[:].rearrange("n u p e -> n (u p e)").bitcast(F32)
-
-        def turn_g_pairs(b, h):
-            g_turned[b, h] = bank_tile([P, 2, P])
-            for u in range(2):
-                nc.tensor.transpose(g_turned[b, h][:, u, :], g_pairs[b, h][:, rows(u)], ident[:])
-
-        def join_turned_g(b, h, engine):
-            new_tile, copy = engine
-            g_words[b, h] = new_tile([P, P, SLOTS], BF16)
-            copy(
-                g_words[b, h][:].rearrange("p n s -> p (n s)").bitcast(F32).rearrange("p (n u) -> p n u", u=2),
-                g_turned[b, h][:].rearrange("p u n -> p n u"),
-            )
+        def words_of(b, h, new_tile):
+            if b % 2 == 0:
+                g_words[b // 2, h] = new_tile([P, 2 * P, SLOTS], BF16)
+            return g_words[b // 2, h][:, rows(b % 2), :]
 
         def weigh_on_vector(b, h):
-            g_words[b, h] = vector_tile([P, P, SLOTS], BF16)
             nc.vector.tensor_tensor(
-                g_words[b, h][:],
+                words_of(b, h, vector_tile),
                 e_bank[b, h][:].rearrange("p s n -> p n s"),
                 weight[:, h, :].unsqueeze(1).to_broadcast([P, P, SLOTS]),
                 MULT,
@@ -201,17 +173,19 @@ def tile_attend_gvq_cw_w_kernel(tc, zT, cb, tw, xT, offs, out):
 
         def join_pairs(b, h, engine):
             new_tile, copy = engine
-            g_words[b, h] = new_tile([P, P, SLOTS], BF16)
-            joined = g_words[b, h][:].rearrange("p n s -> p (n s)").bitcast(F32)
+            joined = words_of(b, h, new_tile).rearrange("p n s -> p (n s)").bitcast(F32)
             copy(
                 joined.rearrange("p (n u) -> p n u", u=2), g_pairs[b, h].rearrange("p (u n) -> p n u", u=2)
             )
 
-        def quantize_g(b, h):
+        def quantize_g_pair(b, h):
+            if b == 0:
+                g_codes[h] = vector_tile([P, DV], U32)
+            columns = slice(b * P, (b + 2) * P)
             nc.vector.quantize_mx(
-                out=g_codes[h][:, rows(b)].bitcast(E5M2),
-                scales=g_scales[h][:, rows(b)],
-                in_=g_words[b, h][:].rearrange("p n s -> p (n s)"),
+                out=g_codes[h][:, columns].bitcast(E5M2),
+                scales=g_scales[h][:, columns],
+                in_=g_words[b // 2, h][:].rearrange("p n s -> p (n s)"),
             )
 
         x_pairs = {}
@@ -237,6 +211,12 @@ def tile_attend_gvq_cw_w_kernel(tc, zT, cb, tw, xT, offs, out):
             for h in range(halves):
                 for u in range(2):
                     nc.tensor.transpose(bank[:, h, u, :], x_pairs[j, h0 + h, u], ident[:])
+
+        def turn_x_half(j, h):
+            if h == 0:
+                x_turned[j, 0] = bank_tile([P, HALVES, 2, P])
+            for u in range(2):
+                nc.tensor.transpose(x_turned[j, 0][:, h, u, :], x_pairs[j, h, u], ident[:])
 
         def join_x(j, h0, halves, engine):
             new_tile, copy = engine
@@ -290,74 +270,59 @@ def tile_attend_gvq_cw_w_kernel(tc, zT, cb, tw, xT, offs, out):
                 copy(result[:], sums[j][:, k * width : (k + 1) * width])
                 nc.sync.dma_start(out[rows(j), k * width : (k + 1) * width], result[:])
 
-        for b in range(2):
+        for b in range(LAST):
             gather_minus(b, 0)
             add_turned('z', b, 0)
             add_turned('d', b, 0)
             gather(b, 1)
             turn_e(b, 1)
+            if b == 2:
+                for h in range(HALVES):
+                    quantize_g_pair(0, h)
             for h in range(2):
                 weigh_on_scalar(b, h)
-                if b > 0:
-                    join_pairs(0, h, on_vector)
-            if b > 0:
-                for h in range(HALVES):
-                    quantize_g(0, h)
-            if b == 0:
-                spread_weights(1)
-        gather_minus(2, 0)
-        add_turned('z', 2, 0)
-        add_turned('d', 2, 0)
-        gather(2, 1)
-        round_x(0,0,2,on_scalar)
-        join_pairs(1,0,on_vector)
-        weigh_rows(2,1)
-        turn_g_pairs(2,1)
-        turn_x(0,0,2)
-        join_pairs(1,1,on_vector)
-        quantize_g(1,0)
-        quantize_g(1,1)
-        weigh_on_scalar(2,0)
-        join_turned_g(2,1,on_vector)
+            for h in range(2):
+                join_pairs(b, h, on_scalar)
         gather_minus(3, 0)
         add_turned('z', 3, 0)
         add_turned('d', 3, 0)
-        join_x(0,0,2,on_scalar)
         gather(3, 1)
-        warm_up()
-        warm_up()
-        round_x(1, 0, HALVES, on_scalar)
-        join_pairs(2,0,on_vector)
-        quantize_g(2, 1)
-        weigh_rows(3,1)
-        turn_g_pairs(3,1)
-        turn_x(1,0,2)
+        turn_e(3, 1)
+        round_x(0,0,1,on_scalar)
+        turn_x_half(0,0)
+        round_x(0,1,1,on_scalar)
+        turn_x_half(0,1)
         weigh_on_vector(3,0)
-        round_x(2, 0, HALVES, on_scalar)
+        quantize_g_pair(2, 0)
+        weigh_on_vector(3,1)
+        round_x(1, 0, HALVES, on_scalar)
+        warm_up()
+        warm_up()
+        turn_x(1,0,2)
+        quantize_g_pair(2, 1)
+        round_x(2, 0, 1, on_scalar)
+        round_x(2, 1, 1, on_vector)
         turn_x(2,0,2)
-        quantize_g(2, 0)
-        quantize_x(0, 0, HALVES)
-        quantize_g(3, 0)
-        join_turned_g(3,1,on_vector)
+        join_x(0,0,2,on_scalar)
         round_x(3, 0, 1, on_vector)
-        quantize_g(3, 1)
         round_x(3, 1, 1, on_vector)
-        product(0, 0)
-        product(0, 1)
         turn_x(3,0,2)
+        quantize_x(0, 0, HALVES)
         join_x(1,0,2,on_scalar)
         join_x(2,0,2,on_scalar)
+        product(0, 0)
+        product(0, 1)
         quantize_x(1, 0, HALVES)
+        join_x(3,0,2,on_scalar)
         product(1, 0)
         product(1, 1)
-        store(0, on_vector)
-        join_x(3,0,2,on_scalar)
         quantize_x(2, 0, HALVES)
+        store(0, on_scalar)
+        quantize_x(3, 0, HALVES)
         product(2, 0)
         product(2, 1)
-        quantize_x(3, 0, HALVES)
-        store(1, on_scalar)
         product(3, 0)
         product(3, 1)
-        store(2, on_vector)
-        store(3, on_scalar)
+        store(1, on_vector)
+        store(2, on_scalar)
+        store(3, on_vector)

@@ -84,14 +84,18 @@ def tile_attend_gvq_cw_w_kernel(tc, zT, cb, tw, xT, offs, out):
             nc.sync.dma_start(part[:], source[rows(i), h * HALF : (h + 1) * HALF])
             halves[i, h] = part[:]
 
-        tw_sb = keep.tile([P, HALVES, 2 * SLOTS], F32, name="tw_sb")
-        nc.scalar.dma_start(tw_sb[:, :, 0:SLOTS], tw[0, :].rearrange("(h p s) -> p h s", h=HALVES, s=SLOTS))
+        tw_row = keep.tile([P, T], F32, name="tw_row")
+        nc.vector.memset(tw_row[:], 0.0)
+
+        def load_weights():
+            nc.sync.dma_start(tw_row[0:1, :], tw[0:1, :])
 
         load_codebook(0)
+        load_weights()
         load_offsets()
         load_whole('z',0); load_codebook(1); load_whole('z',1); load_codebook(2); load_whole('z',2)
         load_codebook(3)
-        load_half('z',3,0); load_half('z',3,1)
+        load_whole('z',3)
         load_whole('x',0)
         load_whole('x',1);load_whole('x',2)
         load_half('x',3,0); load_half('x',3,1)
@@ -99,8 +103,11 @@ def tile_attend_gvq_cw_w_kernel(tc, zT, cb, tw, xT, offs, out):
         ident = keep.tile([P, P], F32, name="ident")
         make_identity(nc, ident[:])
         weight = keep.tile([P, HALVES, SLOTS], F32, name="weight")
-        nc.scalar.activation(weight[:, 0, :], tw_sb[:, 0, 0:SLOTS], COPY, scale=BETA)
-        nc.scalar.activation(weight[:, 1, :], tw_sb[:, 1, 0:SLOTS], COPY, scale=-BETA)
+        for h, factor in enumerate((BETA, -BETA)):
+            tw_bank = bank_tile([P, SLOTS, P])
+            for s in range(SLOTS):
+                nc.tensor.transpose(tw_bank[:, s, :], tw_row[:, h * HALF + s : (h + 1) * HALF : SLOTS], ident[:])
+            nc.scalar.activation(weight[:, h, :], tw_bank[:, :, 0], COPY, scale=factor)
 
         ones = keep.tile([P, DV * SLOTS], BF16, name="ones", align_bytes=ALIGN)
         nc.vector.memset(ones[:], 1.0)
@@ -227,6 +234,15 @@ def tile_attend_gvq_cw_w_kernel(tc, zT, cb, tw, xT, offs, out):
                 bank[:].rearrange("p h u d -> p h d u"),
             )
 
+        def join_x_half(j, h, engine):
+            new_tile, copy = engine
+            if (j, 0) not in x_words:
+                x_words[j, 0] = new_tile([P, HALVES * HALF], BF16)
+            copy(
+                x_words[j, 0][:, h * HALF : (h + 1) * HALF].bitcast(F32).rearrange("p (d u) -> p d u", u=2),
+                x_turned[j, h][:, 0].rearrange("p u d -> p d u"),
+            )
+
         def quantize_x(j, h0, halves):
             codes = vector_tile([P, halves * P], U32)
             scales = keep.tile([P, halves * P], U8, name="x_scales%d_%d" % (j, h0), align_bytes=ALIGN)
@@ -306,14 +322,16 @@ def tile_attend_gvq_cw_w_kernel(tc, zT, cb, tw, xT, offs, out):
         join_x(0,0,2,on_scalar)
         round_x(3, 0, 1, on_vector)
         round_x(3, 1, 1, on_vector)
-        turn_x(3,0,2)
+        turn_x(3,0,1)
+        turn_x(3,1,1)
         quantize_x(0, 0, HALVES)
         join_x(1,0,2,on_scalar)
         join_x(2,0,2,on_scalar)
         product(0, 0)
         product(0, 1)
         quantize_x(1, 0, HALVES)
-        join_x(3,0,2,on_scalar)
+        join_x_half(3,1,on_vector)
+        join_x_half(3,0,on_scalar)
         product(1, 0)
         product(1, 1)
         quantize_x(2, 0, HALVES)

@@ -27,8 +27,8 @@ LIST_COLS = HALF // 16
 LAST = 3
 PSUM_BANKS = 8
 ALIGN = 64
-VECTOR_TILES = 32
-SCALAR_TILES = 24
+VECTOR_BUFFERS = 32
+SCALAR_BUFFERS = 24
 
 
 def tile_attend_gvq_cw_w_kernel(tc, zT, cb, tw, xT, offs, out):
@@ -36,8 +36,8 @@ def tile_attend_gvq_cw_w_kernel(tc, zT, cb, tw, xT, offs, out):
     with ExitStack() as ctx:
         keep = ctx.enter_context(tc.tile_pool(name="keep", bufs=1))
         psum = ctx.enter_context(tc.psum_pool(name="psum", bufs=PSUM_BANKS))
-        vector_pool = ctx.enter_context(tc.tile_pool(name="by_vector", bufs=VECTOR_TILES))
-        scalar_pool = ctx.enter_context(tc.tile_pool(name="by_scalar", bufs=SCALAR_TILES))
+        vector_pool = ctx.enter_context(tc.tile_pool(name="by_vector", bufs=VECTOR_BUFFERS))
+        scalar_pool = ctx.enter_context(tc.tile_pool(name="by_scalar", bufs=SCALAR_BUFFERS))
 
         def vector_tile(shape, dtype):
             return vector_pool.tile(shape, dtype, name="made", tag="made", align_bytes=ALIGN)
@@ -54,6 +54,9 @@ def tile_attend_gvq_cw_w_kernel(tc, zT, cb, tw, xT, offs, out):
         def rows(i):
             return slice(i * P, (i + 1) * P)
 
+        def tokens(h):
+            return slice(h * HALF, (h + 1) * HALF)
+
         offsets = keep.tile([P, T // 16], U16, name="offsets")
         codebook = {}
         z_half = {}
@@ -64,44 +67,33 @@ def tile_attend_gvq_cw_w_kernel(tc, zT, cb, tw, xT, offs, out):
             codebook[b] = keep.tile([P, C], F32, name="cb%d" % b)
             nc.sync.dma_start(codebook[b][:], cb[rows(b), :])
 
-        sources = {"z": (zT, z_half), "x": (xT, x_half)}
-
-        def load_offsets():
-            nc.sync.dma_start(offsets[:], offs)
-
-        def load_whole(name, i):
-            source, halves = sources[name]
+        def load_whole(source, name, i, halves):
             whole = keep.tile([P, T], F32, name="%s%d" % (name, i))
             nc.sync.dma_start(whole[:], source[rows(i), :])
             for h in range(HALVES):
-                halves[i, h] = whole[:, h * HALF : (h + 1) * HALF]
-            if name == "x":
-                x_whole[i] = whole[:]
-
-        def load_half(name, i, h):
-            source, halves = sources[name]
-            part = keep.tile([P, HALF], F32, name="%s%d_%d" % (name, i, h))
-            nc.sync.dma_start(part[:], source[rows(i), h * HALF : (h + 1) * HALF])
-            halves[i, h] = part[:]
+                halves[i, h] = whole[:, tokens(h)]
+            return whole[:]
 
         tw_row = keep.tile([P, T], F32, name="tw_row")
         nc.vector.memset(tw_row[:], 0.0)
 
-        def load_weights():
-            nc.sync.dma_start(tw_row[0:1, :], tw[0:1, :])
-
         load_codebook(0)
-        load_weights()
-        load_offsets()
-        load_whole('z',0); load_codebook(1); load_whole('z',1); load_codebook(2); load_whole('z',2)
-        load_codebook(3)
-        load_whole('z',3)
-        load_whole('x',0)
-        load_whole('x',1);load_whole('x',2)
-        load_half('x',3,0); load_half('x',3,1)
+        nc.sync.dma_start(tw_row[0:1, :], tw[0:1, :])
+        nc.sync.dma_start(offsets[:], offs)
+        for b in range(LAST):
+            load_whole(zT, "z", b, z_half)
+            load_codebook(b + 1)
+        load_whole(zT, "z", LAST, z_half)
+        for j in range(LAST):
+            x_whole[j] = load_whole(xT, "x", j, x_half)
+        for h in range(HALVES):
+            part = keep.tile([P, HALF], F32, name="x%d_%d" % (LAST, h))
+            nc.sync.dma_start(part[:], xT[rows(LAST), tokens(h)])
+            x_half[LAST, h] = part[:]
 
         ident = keep.tile([P, P], F32, name="ident")
         make_identity(nc, ident[:])
+
         weight = keep.tile([P, HALVES, SLOTS], F32, name="weight")
         for h, factor in enumerate((BETA, -BETA)):
             tw_bank = bank_tile([P, SLOTS, P])
@@ -120,55 +112,34 @@ def tile_attend_gvq_cw_w_kernel(tc, zT, cb, tw, xT, offs, out):
 
         g_codes = {}
         g_scales = [keep.tile([P, DV], U8, name="g_scales%d" % h, align_bytes=ALIGN) for h in range(HALVES)]
-        minus_e = {}
         e_bank = {}
         g_pairs = {}
         g_words = {}
 
-        def gather(b, h):
-            picked = vector_tile([P, HALF], F32)
-            listed = offsets[:, h * LIST_COLS : (h + 1) * LIST_COLS]
-            nc.vector.tensor_tensor(picked[:], codebook[b][:].indirect(listed), z_half[b, h], SUBTRACT)
-            minus_e[b, h] = picked[:]
+        def listed(b, h):
+            return codebook[b][:].indirect(offsets[:, h * LIST_COLS : (h + 1) * LIST_COLS])
 
-        def gather_minus(b, h):
-            picked = vector_tile([P, HALF], F32)
-            listed = offsets[:, h * LIST_COLS : (h + 1) * LIST_COLS]
-            nc.vector.tensor_scalar(picked[:], codebook[b][:].indirect(listed), -1.0, 0.0, MULT, ADD)
-            minus_e[b, h] = picked[:]
+        def first_half(b):
+            minus_c = vector_tile([P, HALF], F32)
+            nc.vector.tensor_scalar(minus_c[:], listed(b, 0), -1.0, 0.0, MULT, ADD)
+            e_bank[b, 0] = bank_tile([P, SLOTS, P])
+            for term, source in enumerate((z_half[b, 0], minus_c[:])):
+                for s in range(SLOTS):
+                    nc.tensor.matmul(
+                        e_bank[b, 0][:, s, :],
+                        lhsT=source[:, s:HALF:SLOTS],
+                        rhs=ident[:],
+                        is_transpose=True,
+                        start=term == 0 and s == 0,
+                        stop=term == 1 and s == SLOTS - 1,
+                    )
 
-        def add_turned(name, b, h):
-            source = z_half if name == "z" else minus_e
-            first = (b, h) not in e_bank
-            if first:
-                e_bank[b, h] = bank_tile([P, SLOTS, P])
+        def second_half(b):
+            minus_e = vector_tile([P, HALF], F32)
+            nc.vector.tensor_tensor(minus_e[:], listed(b, 1), z_half[b, 1], SUBTRACT)
+            e_bank[b, 1] = bank_tile([P, SLOTS, P])
             for s in range(SLOTS):
-                nc.tensor.matmul(
-                    e_bank[b, h][:, s, :],
-                    lhsT=source[b, h][:, s:HALF:SLOTS],
-                    rhs=ident[:],
-                    is_transpose=True,
-                    start=first and s == 0,
-                    stop=not first and s == SLOTS - 1,
-                )
-
-        def turn_e(b, h):
-            e_bank[b, h] = bank_tile([P, SLOTS, P])
-            for s in range(SLOTS):
-                nc.tensor.transpose(e_bank[b, h][:, s, :], minus_e[b, h][:, s:HALF:SLOTS], ident[:])
-
-        def words_of(b, h, new_tile):
-            if b % 2 == 0:
-                g_words[b // 2, h] = new_tile([P, 2 * P, SLOTS], BF16)
-            return g_words[b // 2, h][:, rows(b % 2), :]
-
-        def weigh_on_vector(b, h):
-            nc.vector.tensor_tensor(
-                words_of(b, h, vector_tile),
-                e_bank[b, h][:].rearrange("p s n -> p n s"),
-                weight[:, h, :].unsqueeze(1).to_broadcast([P, P, SLOTS]),
-                MULT,
-            )
+                nc.tensor.transpose(e_bank[b, 1][:, s, :], minus_e[:, s:HALF:SLOTS], ident[:])
 
         def weigh_on_scalar(b, h):
             pairs = scalar_tile([P, 2, P, 2], BF16)
@@ -178,14 +149,23 @@ def tile_attend_gvq_cw_w_kernel(tc, zT, cb, tw, xT, offs, out):
                 )
             g_pairs[b, h] = pairs[:].rearrange("p u n e -> p (u n e)").bitcast(F32)
 
-        def join_pairs(b, h, engine):
-            new_tile, copy = engine
-            joined = words_of(b, h, new_tile).rearrange("p n s -> p (n s)").bitcast(F32)
-            copy(
+        def join_g(b, h):
+            if b % 2 == 0:
+                g_words[b // 2, h] = scalar_tile([P, 2 * P, SLOTS], BF16)
+            joined = g_words[b // 2, h][:, rows(b % 2), :].rearrange("p n s -> p (n s)").bitcast(F32)
+            nc.scalar.copy(
                 joined.rearrange("p (n u) -> p n u", u=2), g_pairs[b, h].rearrange("p (u n) -> p n u", u=2)
             )
 
-        def quantize_g_pair(b, h):
+        def weigh_on_vector(b, h):
+            nc.vector.tensor_tensor(
+                g_words[b // 2, h][:, rows(b % 2), :],
+                e_bank[b, h][:].rearrange("p s n -> p n s"),
+                weight[:, h, :].unsqueeze(1).to_broadcast([P, P, SLOTS]),
+                MULT,
+            )
+
+        def quantize_g(b, h):
             if b == 0:
                 g_codes[h] = vector_tile([P, DV], U32)
             columns = slice(b * P, (b + 2) * P)
@@ -196,76 +176,77 @@ def tile_attend_gvq_cw_w_kernel(tc, zT, cb, tw, xT, offs, out):
             )
 
         x_pairs = {}
+        x_bank = {}
         x_words = {}
         x_codes = {}
         x_scales = {}
 
-        def round_x(j, h0, halves, engine):
+        def round_x(j, first, source, engine):
             new_tile, copy = engine
-            source = x_whole[j] if halves == HALVES else x_half[j, h0]
+            halves = source.shape[1] // HALF
             pairs = new_tile([P, 2, halves * P, 2], BF16)
             copy(pairs[:], source.rearrange("d (q u e) -> d u q e", u=2, e=2))
             words = pairs[:].rearrange("d u q e -> d (u q e)").bitcast(F32)
             for u in range(2):
                 for h in range(halves):
-                    x_pairs[j, h0 + h, u] = words[:, rows(u * halves + h)]
+                    x_pairs[j, first + h, u] = words[:, rows(u * halves + h)]
 
-        x_turned = {}
-
-        def turn_x(j, h0, halves):
-            bank = bank_tile([P, halves, 2, P])
-            x_turned[j, h0] = bank
-            for h in range(halves):
-                for u in range(2):
-                    nc.tensor.transpose(bank[:, h, u, :], x_pairs[j, h0 + h, u], ident[:])
+        def round_x_half(j, h, engine):
+            round_x(j, h, x_half[j, h], engine)
 
         def turn_x_half(j, h):
             if h == 0:
-                x_turned[j, 0] = bank_tile([P, HALVES, 2, P])
+                x_bank[j, 0] = bank_tile([P, HALVES, 2, P])
             for u in range(2):
-                nc.tensor.transpose(x_turned[j, 0][:, h, u, :], x_pairs[j, h, u], ident[:])
+                nc.tensor.transpose(x_bank[j, 0][:, h, u, :], x_pairs[j, h, u], ident[:])
 
-        def join_x(j, h0, halves, engine):
-            new_tile, copy = engine
-            bank = x_turned[j, h0]
-            x_words[j, h0] = new_tile([P, halves * HALF], BF16)
-            copy(
-                x_words[j, h0][:].bitcast(F32).rearrange("p (h d u) -> p h d u", h=halves, u=2),
-                bank[:].rearrange("p h u d -> p h d u"),
+        def turn_x(j):
+            for h in range(HALVES):
+                turn_x_half(j, h)
+
+        def turn_x_apart(j):
+            for h in range(HALVES):
+                x_bank[j, h] = bank_tile([P, 1, 2, P])
+                for u in range(2):
+                    nc.tensor.transpose(x_bank[j, h][:, 0, u, :], x_pairs[j, h, u], ident[:])
+
+        def join_x(j):
+            x_words[j] = scalar_tile([P, T], BF16)
+            nc.scalar.copy(
+                x_words[j][:].bitcast(F32).rearrange("p (h d u) -> p h d u", h=HALVES, u=2),
+                x_bank[j, 0][:].rearrange("p h u d -> p h d u"),
             )
 
-        def join_x_half(j, h, engine):
-            new_tile, copy = engine
-            if (j, 0) not in x_words:
-                x_words[j, 0] = new_tile([P, HALVES * HALF], BF16)
-            copy(
-                x_words[j, 0][:, h * HALF : (h + 1) * HALF].bitcast(F32).rearrange("p (d u) -> p d u", u=2),
-                x_turned[j, h][:, 0].rearrange("p u d -> p d u"),
-            )
+        def join_x_apart(j):
+            x_words[j] = vector_tile([P, T], BF16)
+            for h, copy in ((1, nc.vector.tensor_copy), (0, nc.scalar.copy)):
+                copy(
+                    x_words[j][:, tokens(h)].bitcast(F32).rearrange("p (d u) -> p d u", u=2),
+                    x_bank[j, h][:, 0].rearrange("p u d -> p d u"),
+                )
 
-        def quantize_x(j, h0, halves):
-            codes = vector_tile([P, halves * P], U32)
-            scales = keep.tile([P, halves * P], U8, name="x_scales%d_%d" % (j, h0), align_bytes=ALIGN)
-            nc.vector.quantize_mx(out=codes[:].bitcast(E4M3), scales=scales[:], in_=x_words[j, h0][:])
-            for h in range(halves):
-                x_codes[j, h0 + h] = codes[:, rows(h)]
-                x_scales[j, h0 + h] = scales[:, rows(h)]
+        def quantize_x(j):
+            codes = vector_tile([P, HALVES * P], U32)
+            scales = keep.tile([P, HALVES * P], U8, name="x_scales%d" % j, align_bytes=ALIGN)
+            nc.vector.quantize_mx(out=codes[:].bitcast(E4M3), scales=scales[:], in_=x_words[j][:])
+            for h in range(HALVES):
+                x_codes[j, h] = codes[:, rows(h)]
+                x_scales[j, h] = scales[:, rows(h)]
 
         sums = {}
 
-        def product(j, h):
-            first = j not in sums
-            if first:
-                sums[j] = bank_tile([P, DV])
-            nc.tensor.matmul_mx(
-                out=sums[j][:],
-                lhsT=x_codes[j, h].bitcast(E4M3),
-                lhsT_scale=x_scales[j, h],
-                rhs=g_codes[h][:].bitcast(E5M2),
-                rhs_scale=g_scales[h][:],
-                start=first,
-                stop=not first,
-            )
+        def product(j):
+            sums[j] = bank_tile([P, DV])
+            for h in range(HALVES):
+                nc.tensor.matmul_mx(
+                    out=sums[j][:],
+                    lhsT=x_codes[j, h].bitcast(E4M3),
+                    lhsT_scale=x_scales[j, h],
+                    rhs=g_codes[h][:].bitcast(E5M2),
+                    rhs_scale=g_scales[h][:],
+                    start=h == 0,
+                    stop=h == HALVES - 1,
+                )
 
         def warm_up():
             nc.tensor.matmul_mx(
@@ -278,69 +259,56 @@ def tile_attend_gvq_cw_w_kernel(tc, zT, cb, tw, xT, offs, out):
                 stop=True,
             )
 
-        def store(j, engine, parts=1):
+        def store(j, engine, queue):
             new_tile, copy = engine
-            width = DV // parts
-            for k in range(parts):
-                result = new_tile([P, width], F32)
-                copy(result[:], sums[j][:, k * width : (k + 1) * width])
-                nc.sync.dma_start(out[rows(j), k * width : (k + 1) * width], result[:])
+            result = new_tile([P, DV], F32)
+            copy(result[:], sums[j][:])
+            queue.dma_start(out[rows(j), :], result[:])
 
         for b in range(LAST):
-            gather_minus(b, 0)
-            add_turned('z', b, 0)
-            add_turned('d', b, 0)
-            gather(b, 1)
-            turn_e(b, 1)
-            if b == 2:
+            first_half(b)
+            second_half(b)
+            if b == LAST - 1:
                 for h in range(HALVES):
-                    quantize_g_pair(0, h)
-            for h in range(2):
+                    quantize_g(0, h)
+            for h in range(HALVES):
                 weigh_on_scalar(b, h)
-            for h in range(2):
-                join_pairs(b, h, on_scalar)
-        gather_minus(3, 0)
-        add_turned('z', 3, 0)
-        add_turned('d', 3, 0)
-        gather(3, 1)
-        turn_e(3, 1)
-        round_x(0,0,1,on_scalar)
-        turn_x_half(0,0)
-        round_x(0,1,1,on_scalar)
-        turn_x_half(0,1)
-        weigh_on_vector(3,0)
-        quantize_g_pair(2, 0)
-        weigh_on_vector(3,1)
-        round_x(1, 0, HALVES, on_scalar)
+            for h in range(HALVES):
+                join_g(b, h)
+
+        first_half(3)
+        second_half(3)
+        for h in range(HALVES):
+            round_x_half(0, h, on_scalar)
+            turn_x_half(0, h)
+        weigh_on_vector(3, 0)
+        quantize_g(2, 0)
+        weigh_on_vector(3, 1)
+        round_x(1, 0, x_whole[1], on_scalar)
         warm_up()
         warm_up()
-        turn_x(1,0,2)
-        quantize_g_pair(2, 1)
-        round_x(2, 0, 1, on_scalar)
-        round_x(2, 1, 1, on_vector)
-        turn_x(2,0,2)
-        join_x(0,0,2,on_scalar)
-        round_x(3, 0, 1, on_vector)
-        round_x(3, 1, 1, on_vector)
-        turn_x(3,0,1)
-        turn_x(3,1,1)
-        quantize_x(0, 0, HALVES)
-        join_x(1,0,2,on_scalar)
-        join_x(2,0,2,on_scalar)
-        product(0, 0)
-        product(0, 1)
-        quantize_x(1, 0, HALVES)
-        join_x_half(3,1,on_vector)
-        join_x_half(3,0,on_scalar)
-        product(1, 0)
-        product(1, 1)
-        quantize_x(2, 0, HALVES)
-        store(0, on_scalar)
-        quantize_x(3, 0, HALVES)
-        product(2, 0)
-        product(2, 1)
-        product(3, 0)
-        product(3, 1)
-        store(1, on_vector)
-        store(2, on_scalar)
-        store(3, on_vector)
+        turn_x(1)
+        quantize_g(2, 1)
+
+        round_x_half(2, 0, on_scalar)
+        round_x_half(2, 1, on_vector)
+        turn_x(2)
+        join_x(0)
+        for h in range(HALVES):
+            round_x_half(3, h, on_vector)
+        turn_x_apart(3)
+        quantize_x(0)
+        join_x(1)
+        join_x(2)
+        product(0)
+        quantize_x(1)
+        join_x_apart(3)
+        product(1)
+        quantize_x(2)
+        store(0, on_scalar, nc.scalar)
+        quantize_x(3)
+        product(2)
+        product(3)
+        store(1, on_vector, nc.sync)
+        store(2, on_scalar, nc.scalar)
+        store(3, on_vector, nc.sync)

@@ -61,6 +61,7 @@ def tile_attend_gvq_cw_w_kernel(tc, zT, cb, tw, xT, offs, out):
         codebook = {}
         z_half = {}
         x_half = {}
+        z_whole = {}
         x_whole = {}
 
         def load_codebook(b):
@@ -81,7 +82,7 @@ def tile_attend_gvq_cw_w_kernel(tc, zT, cb, tw, xT, offs, out):
         nc.sync.dma_start(tw_row[0:1, :], tw[0:1, :])
         nc.sync.dma_start(offsets[:], offs)
         for b in range(LAST):
-            load_whole(zT, "z", b, z_half)
+            z_whole[b] = load_whole(zT, "z", b, z_half)
             load_codebook(b + 1)
         load_whole(zT, "z", LAST, z_half)
         for j in range(LAST):
@@ -100,15 +101,6 @@ def tile_attend_gvq_cw_w_kernel(tc, zT, cb, tw, xT, offs, out):
             for s in range(SLOTS):
                 nc.tensor.transpose(tw_bank[:, s, :], tw_row[:, h * HALF + s : (h + 1) * HALF : SLOTS], ident[:])
             nc.scalar.activation(weight[:, h, :], tw_bank[:, :, 0], COPY, scale=factor)
-
-        ones = keep.tile([P, DV * SLOTS], BF16, name="ones", align_bytes=ALIGN)
-        nc.vector.memset(ones[:], 1.0)
-        warm_moving = keep.tile([P, DV], U32, name="warm_moving", align_bytes=ALIGN)
-        warm_moving_scales = keep.tile([P, DV], U8, name="warm_moving_scales", align_bytes=ALIGN)
-        nc.vector.quantize_mx(out=warm_moving[:].bitcast(E5M2), scales=warm_moving_scales[:], in_=ones[:])
-        warm_fixed = keep.tile([P, P], U32, name="warm_fixed", align_bytes=ALIGN)
-        warm_fixed_scales = keep.tile([P, P], U8, name="warm_fixed_scales", align_bytes=ALIGN)
-        nc.vector.quantize_mx(out=warm_fixed[:].bitcast(E4M3), scales=warm_fixed_scales[:], in_=ones[:, 0:HALF])
 
         g_codes = {}
         g_scales = [keep.tile([P, DV], U8, name="g_scales%d" % h, align_bytes=ALIGN) for h in range(HALVES)]
@@ -248,13 +240,22 @@ def tile_attend_gvq_cw_w_kernel(tc, zT, cb, tw, xT, offs, out):
                     stop=h == HALVES - 1,
                 )
 
+        warm = {}
+
+        def make_warm_up_operand():
+            warm["codes"] = vector_tile([P, DV], U32)
+            warm["scales"] = keep.tile([P, DV], U8, name="warm_scales", align_bytes=ALIGN)
+            nc.vector.quantize_mx(
+                out=warm["codes"][:].bitcast(E4M3), scales=warm["scales"][:], in_=z_whole[0].bitcast(BF16)
+            )
+
         def warm_up():
             nc.tensor.matmul_mx(
                 out=bank_tile([P, DV])[:],
-                lhsT=warm_fixed[:].bitcast(E4M3),
-                lhsT_scale=warm_fixed_scales[:],
-                rhs=warm_moving[:].bitcast(E5M2),
-                rhs_scale=warm_moving_scales[:],
+                lhsT=g_codes[0][:, rows(0)].bitcast(E5M2),
+                lhsT_scale=g_scales[0][:, rows(0)],
+                rhs=warm["codes"][:].bitcast(E4M3),
+                rhs_scale=warm["scales"][:],
                 start=True,
                 stop=True,
             )
@@ -268,6 +269,8 @@ def tile_attend_gvq_cw_w_kernel(tc, zT, cb, tw, xT, offs, out):
         for b in range(LAST):
             first_half(b)
             second_half(b)
+            if b == 0:
+                make_warm_up_operand()
             if b == LAST - 1:
                 for h in range(HALVES):
                     quantize_g(0, h)

@@ -27,7 +27,7 @@ LIST_COLS = HALF // 16
 LAST = 3
 PSUM_BANKS = 8
 ALIGN = 64
-VECTOR_BUFFERS = 32
+VECTOR_BUFFERS = 40
 SCALAR_BUFFERS = 24
 
 
@@ -45,11 +45,15 @@ def tile_attend_gvq_cw_w_kernel(tc, zT, cb, tw, xT, offs, out):
         def scalar_tile(shape, dtype):
             return scalar_pool.tile(shape, dtype, name="made", tag="made", align_bytes=ALIGN)
 
+        def gpsimd_tile(shape, dtype):
+            return keep.tile(shape, dtype, name="by_gpsimd", align_bytes=ALIGN)
+
         def bank_tile(shape):
             return psum.tile(shape, F32, name="bank", tag="bank")
 
         on_vector = (vector_tile, nc.vector.tensor_copy)
         on_scalar = (scalar_tile, nc.scalar.copy)
+        on_gpsimd = (gpsimd_tile, nc.gpsimd.tensor_copy)
 
         def rows(i):
             return slice(i * P, (i + 1) * P)
@@ -141,17 +145,23 @@ def tile_attend_gvq_cw_w_kernel(tc, zT, cb, tw, xT, offs, out):
                 )
             g_pairs[b, h] = pairs[:].rearrange("p u n e -> p (u n e)").bitcast(F32)
 
+        def g_block(b, h):
+            return g_words[0, h][:, rows(b), :] if b < 2 else g_words[b, h][:]
+
         def join_g(b, h):
-            if b % 2 == 0:
-                g_words[b // 2, h] = scalar_tile([P, 2 * P, SLOTS], BF16)
-            joined = g_words[b // 2, h][:, rows(b % 2), :].rearrange("p n s -> p (n s)").bitcast(F32)
+            if b == 0:
+                g_words[b, h] = scalar_tile([P, 2 * P, SLOTS], BF16)
+            if b == 2:
+                g_words[b, h] = vector_tile([P, P, SLOTS], BF16)
+            joined = g_block(b, h).rearrange("p n s -> p (n s)").bitcast(F32)
             nc.scalar.copy(
                 joined.rearrange("p (n u) -> p n u", u=2), g_pairs[b, h].rearrange("p (u n) -> p n u", u=2)
             )
 
         def weigh_on_vector(b, h):
+            g_words[b, h] = vector_tile([P, P, SLOTS], BF16)
             nc.vector.tensor_tensor(
-                g_words[b // 2, h][:, rows(b % 2), :],
+                g_words[b, h][:],
                 e_bank[b, h][:].rearrange("p s n -> p n s"),
                 weight[:, h, :].unsqueeze(1).to_broadcast([P, P, SLOTS]),
                 MULT,
@@ -160,11 +170,11 @@ def tile_attend_gvq_cw_w_kernel(tc, zT, cb, tw, xT, offs, out):
         def quantize_g(b, h):
             if b == 0:
                 g_codes[h] = vector_tile([P, DV], U32)
-            columns = slice(b * P, (b + 2) * P)
+            columns = slice(b * P, b * P + g_words[b, h].shape[1])
             nc.vector.quantize_mx(
                 out=g_codes[h][:, columns].bitcast(E5M2),
                 scales=g_scales[h][:, columns],
-                in_=g_words[b // 2, h][:].rearrange("p n s -> p (n s)"),
+                in_=g_words[b, h][:].rearrange("p n s -> p (n s)"),
             )
 
         x_pairs = {}
@@ -209,13 +219,34 @@ def tile_attend_gvq_cw_w_kernel(tc, zT, cb, tw, xT, offs, out):
                 x_bank[j, 0][:].rearrange("p h u d -> p h d u"),
             )
 
-        def join_x_apart(j):
-            x_words[j] = vector_tile([P, T], BF16)
-            for h, copy in ((1, nc.vector.tensor_copy), (0, nc.scalar.copy)):
-                copy(
-                    x_words[j][:, tokens(h)].bitcast(F32).rearrange("p (d u) -> p d u", u=2),
-                    x_bank[j, h][:, 0].rearrange("p u d -> p d u"),
-                )
+        def join_x_part(j, h, engine):
+            new_tile, copy = engine
+            if h == 0:
+                x_words[j] = new_tile([P, T], BF16)
+            copy(
+                x_words[j][:, tokens(h)].bitcast(F32).rearrange("p (d u) -> p d u", u=2),
+                x_bank[j, h][:, 0].rearrange("p u d -> p d u"),
+            )
+
+        def turn_x_alone(j, h):
+            x_bank[j, h] = bank_tile([P, 1, 2, P])
+            for u in range(2):
+                nc.tensor.transpose(x_bank[j, h][:, 0, u, :], x_pairs[j, h, u], ident[:])
+
+        def join_x_half(j, h, engine):
+            new_tile, copy = engine
+            x_words[j, h] = new_tile([P, HALF], BF16)
+            copy(
+                x_words[j, h][:].bitcast(F32).rearrange("p (d u) -> p d u", u=2),
+                x_bank[j, h][:, 0].rearrange("p u d -> p d u"),
+            )
+
+        def quantize_x_half(j, h):
+            codes = vector_tile([P, P], U32)
+            scales = keep.tile([P, P], U8, name="x_scales%d_%d" % (j, h), align_bytes=ALIGN)
+            nc.vector.quantize_mx(out=codes[:].bitcast(E4M3), scales=scales[:], in_=x_words[j, h][:])
+            x_codes[j, h] = codes[:]
+            x_scales[j, h] = scales[:]
 
         def quantize_x(j):
             codes = vector_tile([P, HALVES * P], U32)
@@ -227,18 +258,22 @@ def tile_attend_gvq_cw_w_kernel(tc, zT, cb, tw, xT, offs, out):
 
         sums = {}
 
+        def product_pass(j, h):
+            if h == 0:
+                sums[j] = bank_tile([P, DV])
+            nc.tensor.matmul_mx(
+                out=sums[j][:],
+                lhsT=x_codes[j, h].bitcast(E4M3),
+                lhsT_scale=x_scales[j, h],
+                rhs=g_codes[h][:].bitcast(E5M2),
+                rhs_scale=g_scales[h][:],
+                start=h == 0,
+                stop=h == HALVES - 1,
+            )
+
         def product(j):
-            sums[j] = bank_tile([P, DV])
             for h in range(HALVES):
-                nc.tensor.matmul_mx(
-                    out=sums[j][:],
-                    lhsT=x_codes[j, h].bitcast(E4M3),
-                    lhsT_scale=x_scales[j, h],
-                    rhs=g_codes[h][:].bitcast(E5M2),
-                    rhs_scale=g_scales[h][:],
-                    start=h == 0,
-                    stop=h == HALVES - 1,
-                )
+                product_pass(j, h)
 
         warm = {}
 
@@ -260,6 +295,15 @@ def tile_attend_gvq_cw_w_kernel(tc, zT, cb, tw, xT, offs, out):
                 stop=True,
             )
 
+        results = {}
+
+        def copy_half(j, half, engine):
+            new_tile, copy = engine
+            if half == 0:
+                results[j] = new_tile([P, DV], F32)
+            columns = slice(half * DV // 2, (half + 1) * DV // 2)
+            copy(results[j][:, columns], sums[j][:, columns])
+
         def store(j, engine, queue):
             new_tile, copy = engine
             result = new_tile([P, DV], F32)
@@ -276,38 +320,48 @@ def tile_attend_gvq_cw_w_kernel(tc, zT, cb, tw, xT, offs, out):
                     quantize_g(0, h)
             for h in range(HALVES):
                 weigh_on_scalar(b, h)
-            for h in range(HALVES):
-                join_g(b, h)
+            if b < LAST - 1:
+                for h in range(HALVES):
+                    join_g(b, h)
 
         first_half(3)
         second_half(3)
         for h in range(HALVES):
+            join_g(2, h)
+        for h in range(HALVES):
+            quantize_g(2, h)
+        for h in range(HALVES):
             round_x_half(0, h, on_scalar)
-            turn_x_half(0, h)
-        weigh_on_vector(3, 0)
-        quantize_g(2, 0)
-        weigh_on_vector(3, 1)
-        round_x(1, 0, x_whole[1], on_scalar)
+            turn_x_alone(0, h)
+        for h in range(HALVES):
+            weigh_on_vector(3, h)
+        for h in range(HALVES):
+            quantize_g(3, h)
+        round_x_half(1, 0, on_scalar)
+        round_x_half(1, 1, on_gpsimd)
         warm_up()
         warm_up()
         turn_x(1)
-        quantize_g(2, 1)
-
+        for h in range(HALVES):
+            join_x_half(0, h, on_scalar)
+        quantize_x_half(0, 0)
+        product_pass(0, 0)
         round_x_half(2, 0, on_scalar)
         round_x_half(2, 1, on_vector)
-        turn_x(2)
-        join_x(0)
-        for h in range(HALVES):
-            round_x_half(3, h, on_vector)
-        turn_x_apart(3)
-        quantize_x(0)
+        turn_x_apart(2)
         join_x(1)
-        join_x(2)
-        product(0)
+        round_x_half(3, 0, on_vector)
+        round_x_half(3, 1, on_vector)
+        quantize_x_half(0, 1)
+        turn_x_apart(3)
+        product_pass(0, 1)
         quantize_x(1)
-        join_x_apart(3)
+        for h in range(HALVES):
+            join_x_part(2, h, on_scalar)
         product(1)
+        join_x_part(3, 0, on_vector)
         quantize_x(2)
+        join_x_part(3, 1, on_scalar)
         store(0, on_scalar, nc.scalar)
         quantize_x(3)
         product(2)

@@ -16,7 +16,6 @@ E4M3 = mybir.dt.float8_e4m3fn_x4
 E5M2 = mybir.dt.float8_e5m2_x4
 MULT = mybir.AluOpType.mult
 SUBTRACT = mybir.AluOpType.subtract
-ADD = mybir.AluOpType.add
 COPY = mybir.ActivationFunctionType.Copy
 
 P = 128
@@ -24,11 +23,12 @@ SLOTS = 4
 HALF = P * SLOTS
 HALVES = T // HALF
 LIST_COLS = HALF // 16
-LAST = 3
+BLOCKS = 4
+LAST = BLOCKS - 1
 PSUM_BANKS = 8
 ALIGN = 64
 VECTOR_BUFFERS = 40
-SCALAR_BUFFERS = 24
+SCALAR_BUFFERS = 28
 
 
 def tile_attend_gvq_cw_w_kernel(tc, zT, cb, tw, xT, offs, out):
@@ -45,15 +45,11 @@ def tile_attend_gvq_cw_w_kernel(tc, zT, cb, tw, xT, offs, out):
         def scalar_tile(shape, dtype):
             return scalar_pool.tile(shape, dtype, name="made", tag="made", align_bytes=ALIGN)
 
-        def gpsimd_tile(shape, dtype):
-            return keep.tile(shape, dtype, name="by_gpsimd", align_bytes=ALIGN)
-
         def bank_tile(shape):
             return psum.tile(shape, F32, name="bank", tag="bank")
 
         on_vector = (vector_tile, nc.vector.tensor_copy)
         on_scalar = (scalar_tile, nc.scalar.copy)
-        on_gpsimd = (gpsimd_tile, nc.gpsimd.tensor_copy)
 
         def rows(i):
             return slice(i * P, (i + 1) * P)
@@ -65,8 +61,6 @@ def tile_attend_gvq_cw_w_kernel(tc, zT, cb, tw, xT, offs, out):
         codebook = {}
         z_half = {}
         x_half = {}
-        z_whole = {}
-        x_whole = {}
 
         def load_codebook(b):
             codebook[b] = keep.tile([P, C], F32, name="cb%d" % b)
@@ -77,104 +71,108 @@ def tile_attend_gvq_cw_w_kernel(tc, zT, cb, tw, xT, offs, out):
             nc.sync.dma_start(whole[:], source[rows(i), :])
             for h in range(HALVES):
                 halves[i, h] = whole[:, tokens(h)]
-            return whole[:]
 
-        tw_row = keep.tile([P, T], F32, name="tw_row")
-        nc.vector.memset(tw_row[:], 0.0)
+        def load_half(source, name, i, h, halves):
+            part = keep.tile([P, HALF], F32, name="%s%d_%d" % (name, i, h))
+            nc.sync.dma_start(part[:], source[rows(i), tokens(h)])
+            halves[i, h] = part[:]
 
+        tw_word = keep.tile([P, HALVES, SLOTS], F32, name="tw_word")
+        nc.scalar.dma_start(tw_word[:], tw[0:1, :].rearrange("o (h p s) -> (o p) h s", h=HALVES, s=SLOTS))
         load_codebook(0)
-        nc.sync.dma_start(tw_row[0:1, :], tw[0:1, :])
         nc.sync.dma_start(offsets[:], offs)
         for b in range(LAST):
-            z_whole[b] = load_whole(zT, "z", b, z_half)
+            load_whole(zT, "z", b, z_half)
             load_codebook(b + 1)
         load_whole(zT, "z", LAST, z_half)
         for j in range(LAST):
-            x_whole[j] = load_whole(xT, "x", j, x_half)
+            load_whole(xT, "x", j, x_half)
         for h in range(HALVES):
-            part = keep.tile([P, HALF], F32, name="x%d_%d" % (LAST, h))
-            nc.sync.dma_start(part[:], xT[rows(LAST), tokens(h)])
-            x_half[LAST, h] = part[:]
+            load_half(xT, "x", LAST, h, x_half)
 
         ident = keep.tile([P, P], F32, name="ident")
         make_identity(nc, ident[:])
 
-        weight = keep.tile([P, HALVES, SLOTS], F32, name="weight")
-        for h, factor in enumerate((BETA, -BETA)):
-            tw_bank = bank_tile([P, SLOTS, P])
-            for s in range(SLOTS):
-                nc.tensor.transpose(tw_bank[:, s, :], tw_row[:, h * HALF + s : (h + 1) * HALF : SLOTS], ident[:])
-            nc.scalar.activation(weight[:, h, :], tw_bank[:, :, 0], COPY, scale=factor)
+        weight_down = scalar_tile([P, SLOTS], F32)
+        nc.scalar.activation(weight_down[:], tw_word[:, 0, :], COPY, scale=BETA)
+        tw_bank = bank_tile([P, SLOTS, P])
+        for s in range(SLOTS):
+            nc.tensor.transpose(tw_bank[:, s, :], tw_word[:, 1, s : s + 1].to_broadcast([P, P]), ident[:])
+        weight_along = scalar_tile([P, 2, P, 2], F32)
+        nc.scalar.activation(
+            weight_along[:], tw_bank[:].rearrange("n (u e) p -> n u p e", u=2), COPY, scale=-BETA
+        )
 
-        g_codes = {}
+        g_codes = [keep.tile([P, DV], U32, name="g_codes%d" % h, align_bytes=ALIGN) for h in range(HALVES)]
         g_scales = [keep.tile([P, DV], U8, name="g_scales%d" % h, align_bytes=ALIGN) for h in range(HALVES)]
         e_bank = {}
+        looked_up = {}
         g_pairs = {}
+        g_bank = {}
         g_words = {}
 
         def listed(b, h):
             return codebook[b][:].indirect(offsets[:, h * LIST_COLS : (h + 1) * LIST_COLS])
 
-        def first_half(b):
-            minus_c = vector_tile([P, HALF], F32)
-            nc.vector.tensor_scalar(minus_c[:], listed(b, 0), -1.0, 0.0, MULT, ADD)
-            e_bank[b, 0] = bank_tile([P, SLOTS, P])
-            for term, source in enumerate((z_half[b, 0], minus_c[:])):
-                for s in range(SLOTS):
-                    nc.tensor.matmul(
-                        e_bank[b, 0][:, s, :],
-                        lhsT=source[:, s:HALF:SLOTS],
-                        rhs=ident[:],
-                        is_transpose=True,
-                        start=term == 0 and s == 0,
-                        stop=term == 1 and s == SLOTS - 1,
-                    )
-
-        def second_half(b):
-            minus_e = vector_tile([P, HALF], F32)
-            nc.vector.tensor_tensor(minus_e[:], listed(b, 1), z_half[b, 1], SUBTRACT)
-            e_bank[b, 1] = bank_tile([P, SLOTS, P])
+        def add_turned(b, source, first):
             for s in range(SLOTS):
-                nc.tensor.transpose(e_bank[b, 1][:, s, :], minus_e[:, s:HALF:SLOTS], ident[:])
-
-        def weigh_on_scalar(b, h):
-            pairs = scalar_tile([P, 2, P, 2], BF16)
-            for s in range(SLOTS):
-                nc.scalar.activation(
-                    pairs[:, s // 2, :, s % 2], e_bank[b, h][:, s, :], COPY, scale=weight[:, h, s : s + 1]
+                nc.tensor.matmul(
+                    e_bank[b][:, s, :],
+                    lhsT=source[:, s:HALF:SLOTS],
+                    rhs=ident[:],
+                    is_transpose=True,
+                    start=first and s == 0,
+                    stop=not first and s == SLOTS - 1,
                 )
-            g_pairs[b, h] = pairs[:].rearrange("p u n e -> p (u n e)").bitcast(F32)
 
-        def g_block(b, h):
-            return g_words[0, h][:, rows(b), :] if b < 2 else g_words[b, h][:]
+        def turn_z(b):
+            e_bank[b] = bank_tile([P, SLOTS, P])
+            add_turned(b, z_half[b, 0], True)
 
-        def join_g(b, h):
-            if b == 0:
-                g_words[b, h] = scalar_tile([P, 2 * P, SLOTS], BF16)
-            if b == 2:
-                g_words[b, h] = vector_tile([P, P, SLOTS], BF16)
-            joined = g_block(b, h).rearrange("p n s -> p (n s)").bitcast(F32)
-            nc.scalar.copy(
-                joined.rearrange("p (n u) -> p n u", u=2), g_pairs[b, h].rearrange("p (u n) -> p n u", u=2)
-            )
+        def gather_on_scalar(b):
+            looked_up[b, 0] = scalar_tile([P, HALF], F32)
+            nc.scalar.activation(looked_up[b, 0][:], listed(b, 0), COPY, scale=-1.0)
 
-        def weigh_on_vector(b, h):
-            g_words[b, h] = vector_tile([P, P, SLOTS], BF16)
+        def turn_c(b):
+            add_turned(b, looked_up[b, 0][:], False)
+
+        def weigh_turned(b):
+            g_words[b, 0] = vector_tile([P, HALF], BF16)
             nc.vector.tensor_tensor(
-                g_words[b, h][:],
-                e_bank[b, h][:].rearrange("p s n -> p n s"),
-                weight[:, h, :].unsqueeze(1).to_broadcast([P, P, SLOTS]),
+                g_words[b, 0][:].rearrange("p (n s) -> p n s", s=SLOTS),
+                e_bank[b][:].rearrange("p s n -> p n s"),
+                weight_down[:].unsqueeze(1).to_broadcast([P, P, SLOTS]),
                 MULT,
             )
 
+        def gather_on_vector(b):
+            looked_up[b, 1] = vector_tile([P, HALF], F32)
+            nc.vector.tensor_tensor(looked_up[b, 1][:], listed(b, 1), z_half[b, 1], SUBTRACT)
+
+        def weigh_pairs(b):
+            pairs = vector_tile([P, 2, P, 2], BF16)
+            nc.vector.tensor_tensor(
+                pairs[:], looked_up[b, 1][:].rearrange("n (p u e) -> n u p e", u=2, e=2), weight_along[:], MULT
+            )
+            g_pairs[b] = pairs[:].rearrange("n u p e -> n (u p e)").bitcast(F32)
+
+        def turn_pairs(b):
+            g_bank[b] = bank_tile([P, 2, P])
+            for u in range(2):
+                nc.tensor.transpose(g_bank[b][:, u, :], g_pairs[b][:, rows(u)], ident[:])
+
+        def join(bank, engine):
+            new_tile, copy = engine
+            words = new_tile([P, HALF], BF16)
+            copy(words[:].bitcast(F32).rearrange("p (c u) -> p c u", u=2), bank.rearrange("p u c -> p c u"))
+            return words
+
+        def join_g(b, engine):
+            g_words[b, 1] = join(g_bank[b][:], engine)
+
         def quantize_g(b, h):
-            if b == 0:
-                g_codes[h] = vector_tile([P, DV], U32)
-            columns = slice(b * P, b * P + g_words[b, h].shape[1])
             nc.vector.quantize_mx(
-                out=g_codes[h][:, columns].bitcast(E5M2),
-                scales=g_scales[h][:, columns],
-                in_=g_words[b, h][:].rearrange("p n s -> p (n s)"),
+                out=g_codes[h][:, rows(b)].bitcast(E5M2), scales=g_scales[h][:, rows(b)], in_=g_words[b, h][:]
             )
 
         x_pairs = {}
@@ -183,78 +181,26 @@ def tile_attend_gvq_cw_w_kernel(tc, zT, cb, tw, xT, offs, out):
         x_codes = {}
         x_scales = {}
 
-        def round_x(j, first, source, engine):
+        def round_x(j, h, engine):
             new_tile, copy = engine
-            halves = source.shape[1] // HALF
-            pairs = new_tile([P, 2, halves * P, 2], BF16)
-            copy(pairs[:], source.rearrange("d (q u e) -> d u q e", u=2, e=2))
-            words = pairs[:].rearrange("d u q e -> d (u q e)").bitcast(F32)
+            pairs = new_tile([P, 2, P, 2], BF16)
+            copy(pairs[:], x_half[j, h].rearrange("d (p u e) -> d u p e", u=2, e=2))
+            x_pairs[j, h] = pairs[:].rearrange("d u p e -> d (u p e)").bitcast(F32)
+
+        def turn_x(j, h):
+            x_bank[j, h] = bank_tile([P, 2, P])
             for u in range(2):
-                for h in range(halves):
-                    x_pairs[j, first + h, u] = words[:, rows(u * halves + h)]
+                nc.tensor.transpose(x_bank[j, h][:, u, :], x_pairs[j, h][:, rows(u)], ident[:])
 
-        def round_x_half(j, h, engine):
-            round_x(j, h, x_half[j, h], engine)
+        def join_x(j, h, engine):
+            x_words[j, h] = join(x_bank[j, h][:], engine)
 
-        def turn_x_half(j, h):
-            if h == 0:
-                x_bank[j, 0] = bank_tile([P, HALVES, 2, P])
-            for u in range(2):
-                nc.tensor.transpose(x_bank[j, 0][:, h, u, :], x_pairs[j, h, u], ident[:])
-
-        def turn_x(j):
-            for h in range(HALVES):
-                turn_x_half(j, h)
-
-        def turn_x_apart(j):
-            for h in range(HALVES):
-                x_bank[j, h] = bank_tile([P, 1, 2, P])
-                for u in range(2):
-                    nc.tensor.transpose(x_bank[j, h][:, 0, u, :], x_pairs[j, h, u], ident[:])
-
-        def join_x(j):
-            x_words[j] = scalar_tile([P, T], BF16)
-            nc.scalar.copy(
-                x_words[j][:].bitcast(F32).rearrange("p (h d u) -> p h d u", h=HALVES, u=2),
-                x_bank[j, 0][:].rearrange("p h u d -> p h d u"),
-            )
-
-        def join_x_part(j, h, engine):
-            new_tile, copy = engine
-            if h == 0:
-                x_words[j] = new_tile([P, T], BF16)
-            copy(
-                x_words[j][:, tokens(h)].bitcast(F32).rearrange("p (d u) -> p d u", u=2),
-                x_bank[j, h][:, 0].rearrange("p u d -> p d u"),
-            )
-
-        def turn_x_alone(j, h):
-            x_bank[j, h] = bank_tile([P, 1, 2, P])
-            for u in range(2):
-                nc.tensor.transpose(x_bank[j, h][:, 0, u, :], x_pairs[j, h, u], ident[:])
-
-        def join_x_half(j, h, engine):
-            new_tile, copy = engine
-            x_words[j, h] = new_tile([P, HALF], BF16)
-            copy(
-                x_words[j, h][:].bitcast(F32).rearrange("p (d u) -> p d u", u=2),
-                x_bank[j, h][:, 0].rearrange("p u d -> p d u"),
-            )
-
-        def quantize_x_half(j, h):
+        def quantize_x(j, h):
             codes = vector_tile([P, P], U32)
             scales = keep.tile([P, P], U8, name="x_scales%d_%d" % (j, h), align_bytes=ALIGN)
             nc.vector.quantize_mx(out=codes[:].bitcast(E4M3), scales=scales[:], in_=x_words[j, h][:])
             x_codes[j, h] = codes[:]
             x_scales[j, h] = scales[:]
-
-        def quantize_x(j):
-            codes = vector_tile([P, HALVES * P], U32)
-            scales = keep.tile([P, HALVES * P], U8, name="x_scales%d" % j, align_bytes=ALIGN)
-            nc.vector.quantize_mx(out=codes[:].bitcast(E4M3), scales=scales[:], in_=x_words[j][:])
-            for h in range(HALVES):
-                x_codes[j, h] = codes[:, rows(h)]
-                x_scales[j, h] = scales[:, rows(h)]
 
         sums = {}
 
@@ -271,38 +217,27 @@ def tile_attend_gvq_cw_w_kernel(tc, zT, cb, tw, xT, offs, out):
                 stop=h == HALVES - 1,
             )
 
-        def product(j):
+        def split_product(j):
+            banks = [bank_tile([P, DV // 2]) for side in range(2)]
             for h in range(HALVES):
-                product_pass(j, h)
+                for side in range(2):
+                    columns = slice(side * DV // 2, (side + 1) * DV // 2)
+                    nc.tensor.matmul_mx(
+                        out=banks[side][:],
+                        lhsT=x_codes[j, h].bitcast(E4M3),
+                        lhsT_scale=x_scales[j, h],
+                        rhs=g_codes[h][:, columns].bitcast(E5M2),
+                        rhs_scale=g_scales[h][:, columns],
+                        start=h == 0,
+                        stop=h == HALVES - 1,
+                    )
+            return banks
 
-        warm = {}
-
-        def make_warm_up_operand():
-            warm["codes"] = vector_tile([P, DV], U32)
-            warm["scales"] = keep.tile([P, DV], U8, name="warm_scales", align_bytes=ALIGN)
-            nc.vector.quantize_mx(
-                out=warm["codes"][:].bitcast(E4M3), scales=warm["scales"][:], in_=z_whole[0].bitcast(BF16)
-            )
-
-        def warm_up():
-            nc.tensor.matmul_mx(
-                out=bank_tile([P, DV])[:],
-                lhsT=g_codes[0][:, rows(0)].bitcast(E5M2),
-                lhsT_scale=g_scales[0][:, rows(0)],
-                rhs=warm["codes"][:].bitcast(E4M3),
-                rhs_scale=warm["scales"][:],
-                start=True,
-                stop=True,
-            )
-
-        results = {}
-
-        def copy_half(j, half, engine):
-            new_tile, copy = engine
-            if half == 0:
-                results[j] = new_tile([P, DV], F32)
-            columns = slice(half * DV // 2, (half + 1) * DV // 2)
-            copy(results[j][:, columns], sums[j][:, columns])
+        def split_store(j, banks, queue):
+            result = vector_tile([P, DV], F32)
+            nc.scalar.copy(result[:, : DV // 2], banks[0][:])
+            nc.vector.tensor_copy(result[:, DV // 2 :], banks[1][:])
+            queue.dma_start(out[rows(j), :], result[:])
 
         def store(j, engine, queue):
             new_tile, copy = engine
@@ -310,62 +245,64 @@ def tile_attend_gvq_cw_w_kernel(tc, zT, cb, tw, xT, offs, out):
             copy(result[:], sums[j][:])
             queue.dma_start(out[rows(j), :], result[:])
 
-        for b in range(LAST):
-            first_half(b)
-            second_half(b)
-            if b == 0:
-                make_warm_up_operand()
-            if b == LAST - 1:
-                for h in range(HALVES):
-                    quantize_g(0, h)
-            for h in range(HALVES):
-                weigh_on_scalar(b, h)
-            if b < LAST - 1:
-                for h in range(HALVES):
-                    join_g(b, h)
-
-        first_half(3)
-        second_half(3)
-        for h in range(HALVES):
-            join_g(2, h)
-        for h in range(HALVES):
-            quantize_g(2, h)
-        for h in range(HALVES):
-            round_x_half(0, h, on_scalar)
-            turn_x_alone(0, h)
-        for h in range(HALVES):
-            weigh_on_vector(3, h)
-        for h in range(HALVES):
-            quantize_g(3, h)
-        round_x_half(1, 0, on_scalar)
-        round_x_half(1, 1, on_gpsimd)
-        warm_up()
-        warm_up()
-        turn_x(1)
-        for h in range(HALVES):
-            join_x_half(0, h, on_scalar)
-        quantize_x_half(0, 0)
+        for b in range(BLOCKS):
+            gather_on_scalar(b)
+            if b > 0:
+                turn_pairs(b - 1)
+                weigh_turned(b - 1)
+                quantize_g(b - 1, 0)
+            turn_z(b)
+            turn_c(b)
+            gather_on_vector(b)
+            if b > 0:
+                join_g(b - 1, (vector_tile, nc.scalar.copy))
+                quantize_g(b - 1, 1)
+            weigh_pairs(b)
+        round_x(0, 0, on_scalar)
+        round_x(0, 1, on_scalar)
+        turn_x(0, 0)
+        turn_pairs(LAST)
+        turn_x(0, 1)
+        weigh_turned(LAST)
+        round_x(1, 0, on_scalar)
+        join_x(0, 0, on_scalar)
+        join_g(LAST, on_scalar)
+        join_x(0, 1, on_scalar)
+        round_x(1, 1, on_vector)
+        quantize_g(LAST, 0)
+        turn_x(1, 0)
+        turn_x(1, 1)
+        round_x(2, 0, on_vector)
+        quantize_x(0, 0)
+        quantize_g(LAST, 1)
+        round_x(2, 1, on_vector)
+        quantize_x(0, 1)
         product_pass(0, 0)
-        round_x_half(2, 0, on_scalar)
-        round_x_half(2, 1, on_vector)
-        turn_x_apart(2)
-        join_x(1)
-        round_x_half(3, 0, on_vector)
-        round_x_half(3, 1, on_vector)
-        quantize_x_half(0, 1)
-        turn_x_apart(3)
         product_pass(0, 1)
-        quantize_x(1)
+        join_x(1, 0, on_scalar)
+        join_x(1, 1, on_scalar)
+        turn_x(2, 0)
+        turn_x(2, 1)
+        round_x(3, 0, on_vector)
+        quantize_x(1, 0)
+        round_x(3, 1, on_vector)
+        quantize_x(1, 1)
+        turn_x(3, 0)
+        turn_x(3, 1)
+        product_pass(1, 0)
+        product_pass(1, 1)
+        store(0, on_scalar, nc.sync)
+        join_x(2, 0, on_vector)
+        join_x(2, 1, on_scalar)
+        join_x(3, 0, on_vector)
+        quantize_x(2, 0)
+        join_x(3, 1, on_scalar)
+        quantize_x(2, 1)
+        quantize_x(3, 0)
+        quantize_x(3, 1)
         for h in range(HALVES):
-            join_x_part(2, h, on_scalar)
-        product(1)
-        join_x_part(3, 0, on_vector)
-        quantize_x(2)
-        join_x_part(3, 1, on_scalar)
-        store(0, on_scalar, nc.scalar)
-        quantize_x(3)
-        product(2)
-        product(3)
-        store(1, on_vector, nc.sync)
-        store(2, on_scalar, nc.scalar)
-        store(3, on_vector, nc.sync)
+            product_pass(2, h)
+        last_banks = split_product(LAST)
+        store(1, on_scalar, nc.sync)
+        store(2, on_vector, nc.sync)
+        split_store(LAST, last_banks, nc.scalar)

@@ -27,29 +27,31 @@ BLOCKS = 4
 LAST = BLOCKS - 1
 PSUM_BANKS = 8
 ALIGN = 64
-VECTOR_BUFFERS = 40
-SCALAR_BUFFERS = 28
+RING_BUFFERS = 64
 
 
 def tile_attend_gvq_cw_w_kernel(tc, zT, cb, tw, xT, offs, out):
     nc = tc.nc
     with ExitStack() as ctx:
         keep = ctx.enter_context(tc.tile_pool(name="keep", bufs=1))
-        psum = ctx.enter_context(tc.psum_pool(name="psum", bufs=PSUM_BANKS))
-        vector_pool = ctx.enter_context(tc.tile_pool(name="by_vector", bufs=VECTOR_BUFFERS))
-        scalar_pool = ctx.enter_context(tc.tile_pool(name="by_scalar", bufs=SCALAR_BUFFERS))
+        psum = ctx.enter_context(tc.psum_pool(name="psum", bufs=PSUM_BANKS - 1))
+        held = ctx.enter_context(tc.psum_pool(name="held", bufs=1))
+        ring = ctx.enter_context(tc.tile_pool(name="ring", bufs=RING_BUFFERS))
 
         def vector_tile(shape, dtype):
-            return vector_pool.tile(shape, dtype, name="made", tag="made", align_bytes=ALIGN)
+            return ring.tile(shape, dtype, name="made", tag="made", align_bytes=ALIGN)
 
-        def scalar_tile(shape, dtype):
-            return scalar_pool.tile(shape, dtype, name="made", tag="made", align_bytes=ALIGN)
+        scalar_tile = vector_tile
+
+        def gpsimd_tile(shape, dtype):
+            return keep.tile(shape, dtype, name="by_gpsimd", align_bytes=ALIGN)
 
         def bank_tile(shape):
             return psum.tile(shape, F32, name="bank", tag="bank")
 
         on_vector = (vector_tile, nc.vector.tensor_copy)
         on_scalar = (scalar_tile, nc.scalar.copy)
+        on_gpsimd = (gpsimd_tile, nc.gpsimd.tensor_copy)
 
         def rows(i):
             return slice(i * P, (i + 1) * P)
@@ -77,9 +79,10 @@ def tile_attend_gvq_cw_w_kernel(tc, zT, cb, tw, xT, offs, out):
             nc.sync.dma_start(part[:], source[rows(i), tokens(h)])
             halves[i, h] = part[:]
 
-        tw_word = keep.tile([P, HALVES, SLOTS], F32, name="tw_word")
-        nc.scalar.dma_start(tw_word[:], tw[0:1, :].rearrange("o (h p s) -> (o p) h s", h=HALVES, s=SLOTS))
+        tw_rows = keep.tile([P, HALF], F32, name="tw_rows")
+        nc.vector.memset(tw_rows[:], 0.0)
         load_codebook(0)
+        nc.sync.dma_start(tw_rows[0:HALVES, :], tw[0:1, :].rearrange("o (h t) -> (o h) t", h=HALVES))
         nc.sync.dma_start(offsets[:], offs)
         for b in range(LAST):
             load_whole(zT, "z", b, z_half)
@@ -93,15 +96,17 @@ def tile_attend_gvq_cw_w_kernel(tc, zT, cb, tw, xT, offs, out):
         ident = keep.tile([P, P], F32, name="ident")
         make_identity(nc, ident[:])
 
-        weight_down = scalar_tile([P, SLOTS], F32)
-        nc.scalar.activation(weight_down[:], tw_word[:, 0, :], COPY, scale=BETA)
         tw_bank = bank_tile([P, SLOTS, P])
         for s in range(SLOTS):
-            nc.tensor.transpose(tw_bank[:, s, :], tw_word[:, 1, s : s + 1].to_broadcast([P, P]), ident[:])
-        weight_along = scalar_tile([P, 2, P, 2], F32)
-        nc.scalar.activation(
-            weight_along[:], tw_bank[:].rearrange("n (u e) p -> n u p e", u=2), COPY, scale=-BETA
-        )
+            nc.tensor.transpose(tw_bank[:, s, :], tw_rows[:, s:HALF:SLOTS], ident[:])
+        minus_weight = scalar_tile([P, SLOTS], F32)
+        nc.scalar.activation(minus_weight[:], tw_bank[:, :, 1], COPY, scale=-BETA)
+        weight_down = scalar_tile([P, SLOTS], F32)
+        nc.scalar.activation(weight_down[:], tw_bank[:, :, 0], COPY, scale=BETA)
+        weight_bank = held.tile([P, SLOTS, P], F32, name="weight_bank")
+        for s in range(SLOTS):
+            nc.tensor.transpose(weight_bank[:, s, :], minus_weight[:, s : s + 1].to_broadcast([P, P]), ident[:])
+        weight_along = weight_bank[:].rearrange("n (u e) p -> n u p e", u=2)
 
         g_codes = [keep.tile([P, DV], U32, name="g_codes%d" % h, align_bytes=ALIGN) for h in range(HALVES)]
         g_scales = [keep.tile([P, DV], U8, name="g_scales%d" % h, align_bytes=ALIGN) for h in range(HALVES)]
@@ -152,7 +157,7 @@ def tile_attend_gvq_cw_w_kernel(tc, zT, cb, tw, xT, offs, out):
         def weigh_pairs(b):
             pairs = vector_tile([P, 2, P, 2], BF16)
             nc.vector.tensor_tensor(
-                pairs[:], looked_up[b, 1][:].rearrange("n (p u e) -> n u p e", u=2, e=2), weight_along[:], MULT
+                pairs[:], looked_up[b, 1][:].rearrange("n (p u e) -> n u p e", u=2, e=2), weight_along, MULT
             )
             g_pairs[b] = pairs[:].rearrange("n u p e -> n (u p e)").bitcast(F32)
 
@@ -217,26 +222,27 @@ def tile_attend_gvq_cw_w_kernel(tc, zT, cb, tw, xT, offs, out):
                 stop=h == HALVES - 1,
             )
 
-        def split_product(j):
-            banks = [bank_tile([P, DV // 2]) for side in range(2)]
-            for h in range(HALVES):
-                for side in range(2):
-                    columns = slice(side * DV // 2, (side + 1) * DV // 2)
-                    nc.tensor.matmul_mx(
-                        out=banks[side][:],
-                        lhsT=x_codes[j, h].bitcast(E4M3),
-                        lhsT_scale=x_scales[j, h],
-                        rhs=g_codes[h][:, columns].bitcast(E5M2),
-                        rhs_scale=g_scales[h][:, columns],
-                        start=h == 0,
-                        stop=h == HALVES - 1,
-                    )
-            return banks
+        halves_of_sums = {}
 
-        def split_store(j, banks, queue):
+        def split_pass(j, h):
+            if h == 0:
+                halves_of_sums[j] = [bank_tile([P, DV // 2]) for side in range(2)]
+            for side in range(2):
+                columns = slice(side * DV // 2, (side + 1) * DV // 2)
+                nc.tensor.matmul_mx(
+                    out=halves_of_sums[j][side][:],
+                    lhsT=x_codes[j, h].bitcast(E4M3),
+                    lhsT_scale=x_scales[j, h],
+                    rhs=g_codes[h][:, columns].bitcast(E5M2),
+                    rhs_scale=g_scales[h][:, columns],
+                    start=h == 0,
+                    stop=h == HALVES - 1,
+                )
+
+        def split_store(j, queue):
             result = vector_tile([P, DV], F32)
-            nc.scalar.copy(result[:, : DV // 2], banks[0][:])
-            nc.vector.tensor_copy(result[:, DV // 2 :], banks[1][:])
+            nc.scalar.copy(result[:, : DV // 2], halves_of_sums[j][0][:])
+            nc.vector.tensor_copy(result[:, DV // 2 :], halves_of_sums[j][1][:])
             queue.dma_start(out[rows(j), :], result[:])
 
         def store(j, engine, queue):
@@ -245,19 +251,26 @@ def tile_attend_gvq_cw_w_kernel(tc, zT, cb, tw, xT, offs, out):
             copy(result[:], sums[j][:])
             queue.dma_start(out[rows(j), :], result[:])
 
+        held_join = (vector_tile, nc.scalar.copy)
         for b in range(BLOCKS):
             gather_on_scalar(b)
             if b > 0:
                 turn_pairs(b - 1)
+            if b > 1:
                 weigh_turned(b - 1)
                 quantize_g(b - 1, 0)
             turn_z(b)
             turn_c(b)
             gather_on_vector(b)
             if b > 0:
-                join_g(b - 1, (vector_tile, nc.scalar.copy))
+                join_g(b - 1, held_join)
+            if b == 1:
+                weigh_turned(b - 1)
+            if b > 0:
                 quantize_g(b - 1, 1)
             weigh_pairs(b)
+            if b == 1:
+                quantize_g(b - 1, 0)
         round_x(0, 0, on_scalar)
         round_x(0, 1, on_scalar)
         turn_x(0, 0)
@@ -265,33 +278,33 @@ def tile_attend_gvq_cw_w_kernel(tc, zT, cb, tw, xT, offs, out):
         turn_x(0, 1)
         weigh_turned(LAST)
         round_x(1, 0, on_scalar)
+        round_x(1, 1, on_gpsimd)
         join_x(0, 0, on_scalar)
         join_g(LAST, on_scalar)
         join_x(0, 1, on_scalar)
-        round_x(1, 1, on_vector)
         quantize_g(LAST, 0)
         turn_x(1, 0)
         turn_x(1, 1)
-        round_x(2, 0, on_vector)
         quantize_x(0, 0)
+        round_x(2, 0, on_vector)
         quantize_g(LAST, 1)
-        round_x(2, 1, on_vector)
         quantize_x(0, 1)
-        product_pass(0, 0)
-        product_pass(0, 1)
         join_x(1, 0, on_scalar)
         join_x(1, 1, on_scalar)
+        round_x(2, 1, on_vector)
+        quantize_x(1, 0)
+        product_pass(0, 0)
+        product_pass(0, 1)
+        split_pass(1, 0)
         turn_x(2, 0)
         turn_x(2, 1)
         round_x(3, 0, on_vector)
-        quantize_x(1, 0)
         round_x(3, 1, on_vector)
         quantize_x(1, 1)
         turn_x(3, 0)
         turn_x(3, 1)
-        product_pass(1, 0)
-        product_pass(1, 1)
         store(0, on_scalar, nc.sync)
+        split_pass(1, 1)
         join_x(2, 0, on_vector)
         join_x(2, 1, on_scalar)
         join_x(3, 0, on_vector)
@@ -300,9 +313,9 @@ def tile_attend_gvq_cw_w_kernel(tc, zT, cb, tw, xT, offs, out):
         quantize_x(2, 1)
         quantize_x(3, 0)
         quantize_x(3, 1)
-        for h in range(HALVES):
-            product_pass(2, h)
-        last_banks = split_product(LAST)
-        store(1, on_scalar, nc.sync)
-        store(2, on_vector, nc.sync)
-        split_store(LAST, last_banks, nc.scalar)
+        for j in (2, 3):
+            for h in range(HALVES):
+                split_pass(j, h)
+        split_store(1, nc.sync)
+        split_store(2, nc.sync)
+        split_store(3, nc.scalar)

@@ -15,7 +15,7 @@ U8 = mybir.dt.uint8
 E4M3 = mybir.dt.float8_e4m3fn_x4
 E5M2 = mybir.dt.float8_e5m2_x4
 MULT = mybir.AluOpType.mult
-SUBTRACT = mybir.AluOpType.subtract
+ADD = mybir.AluOpType.add
 COPY = mybir.ActivationFunctionType.Copy
 
 P = 128
@@ -34,24 +34,18 @@ def tile_attend_gvq_cw_w_kernel(tc, zT, cb, tw, xT, offs, out):
     nc = tc.nc
     with ExitStack() as ctx:
         keep = ctx.enter_context(tc.tile_pool(name="keep", bufs=1))
-        psum = ctx.enter_context(tc.psum_pool(name="psum", bufs=PSUM_BANKS - 1))
-        held = ctx.enter_context(tc.psum_pool(name="held", bufs=1))
+        psum = ctx.enter_context(tc.psum_pool(name="psum", bufs=PSUM_BANKS))
         ring = ctx.enter_context(tc.tile_pool(name="ring", bufs=RING_BUFFERS))
 
-        def vector_tile(shape, dtype):
+        def new_tile(shape, dtype):
             return ring.tile(shape, dtype, name="made", tag="made", align_bytes=ALIGN)
-
-        scalar_tile = vector_tile
-
-        def gpsimd_tile(shape, dtype):
-            return keep.tile(shape, dtype, name="by_gpsimd", align_bytes=ALIGN)
 
         def bank_tile(shape):
             return psum.tile(shape, F32, name="bank", tag="bank")
 
-        on_vector = (vector_tile, nc.vector.tensor_copy)
-        on_scalar = (scalar_tile, nc.scalar.copy)
-        on_gpsimd = (gpsimd_tile, nc.gpsimd.tensor_copy)
+        on_vector = nc.vector.tensor_copy
+        on_scalar = nc.scalar.copy
+        on_gpsimd = nc.gpsimd.tensor_copy
 
         def rows(i):
             return slice(i * P, (i + 1) * P)
@@ -87,7 +81,8 @@ def tile_attend_gvq_cw_w_kernel(tc, zT, cb, tw, xT, offs, out):
         for b in range(LAST):
             load_whole(zT, "z", b, z_half)
             load_codebook(b + 1)
-        load_whole(zT, "z", LAST, z_half)
+        for h in range(HALVES):
+            load_half(zT, "z", LAST, h, z_half)
         for j in range(LAST):
             load_whole(xT, "x", j, x_half)
         for h in range(HALVES):
@@ -99,30 +94,33 @@ def tile_attend_gvq_cw_w_kernel(tc, zT, cb, tw, xT, offs, out):
         tw_bank = bank_tile([P, SLOTS, P])
         for s in range(SLOTS):
             nc.tensor.transpose(tw_bank[:, s, :], tw_rows[:, s:HALF:SLOTS], ident[:])
-        minus_weight = scalar_tile([P, SLOTS], F32)
-        nc.scalar.activation(minus_weight[:], tw_bank[:, :, 1], COPY, scale=-BETA)
-        weight_down = scalar_tile([P, SLOTS], F32)
-        nc.scalar.activation(weight_down[:], tw_bank[:, :, 0], COPY, scale=BETA)
-        weight_bank = held.tile([P, SLOTS, P], F32, name="weight_bank")
-        for s in range(SLOTS):
-            nc.tensor.transpose(weight_bank[:, s, :], minus_weight[:, s : s + 1].to_broadcast([P, P]), ident[:])
-        weight_along = weight_bank[:].rearrange("n (u e) p -> n u p e", u=2)
+        weight = new_tile([P, HALVES, SLOTS], F32)
+        nc.scalar.activation(weight[:], tw_bank[:, :, 0:HALVES].rearrange("p s h -> p h s"), COPY, scale=BETA)
 
         g_codes = [keep.tile([P, DV], U32, name="g_codes%d" % h, align_bytes=ALIGN) for h in range(HALVES)]
         g_scales = [keep.tile([P, DV], U8, name="g_scales%d" % h, align_bytes=ALIGN) for h in range(HALVES)]
         e_bank = {}
-        looked_up = {}
-        g_pairs = {}
-        g_bank = {}
+        minus_c = {}
         g_words = {}
 
         def listed(b, h):
             return codebook[b][:].indirect(offsets[:, h * LIST_COLS : (h + 1) * LIST_COLS])
 
-        def add_turned(b, source, first):
+        def gather_on_vector(b, h):
+            minus_c[b, h] = new_tile([P, HALF], F32)
+            nc.vector.tensor_scalar(minus_c[b, h][:], listed(b, h), -1.0, 0.0, MULT, ADD)
+
+        def gather_on_scalar(b, h):
+            minus_c[b, h] = new_tile([P, HALF], F32)
+            nc.scalar.activation(minus_c[b, h][:], listed(b, h), COPY, scale=-1.0)
+
+        def add_turned(b, h, source):
+            first = (b, h) not in e_bank
+            if first:
+                e_bank[b, h] = bank_tile([P, SLOTS, P])
             for s in range(SLOTS):
                 nc.tensor.matmul(
-                    e_bank[b][:, s, :],
+                    e_bank[b, h][:, s, :],
                     lhsT=source[:, s:HALF:SLOTS],
                     rhs=ident[:],
                     is_transpose=True,
@@ -130,50 +128,25 @@ def tile_attend_gvq_cw_w_kernel(tc, zT, cb, tw, xT, offs, out):
                     stop=not first and s == SLOTS - 1,
                 )
 
-        def turn_z(b):
-            e_bank[b] = bank_tile([P, SLOTS, P])
-            add_turned(b, z_half[b, 0], True)
+        def turn_z(b, h):
+            add_turned(b, h, z_half[b, h])
 
-        def gather_on_scalar(b):
-            looked_up[b, 0] = scalar_tile([P, HALF], F32)
-            nc.scalar.activation(looked_up[b, 0][:], listed(b, 0), COPY, scale=-1.0)
+        def turn_c(b, h):
+            add_turned(b, h, minus_c[b, h][:])
 
-        def turn_c(b):
-            add_turned(b, looked_up[b, 0][:], False)
-
-        def weigh_turned(b):
-            g_words[b, 0] = vector_tile([P, HALF], BF16)
+        def weigh(b, h):
+            g_words[b, h] = new_tile([P, HALF], BF16)
             nc.vector.tensor_tensor(
-                g_words[b, 0][:].rearrange("p (n s) -> p n s", s=SLOTS),
-                e_bank[b][:].rearrange("p s n -> p n s"),
-                weight_down[:].unsqueeze(1).to_broadcast([P, P, SLOTS]),
+                g_words[b, h][:].rearrange("p (n s) -> p n s", s=SLOTS),
+                e_bank[b, h][:].rearrange("p s n -> p n s"),
+                weight[:, h, :].unsqueeze(1).to_broadcast([P, P, SLOTS]),
                 MULT,
             )
 
-        def gather_on_vector(b):
-            looked_up[b, 1] = vector_tile([P, HALF], F32)
-            nc.vector.tensor_tensor(looked_up[b, 1][:], listed(b, 1), z_half[b, 1], SUBTRACT)
-
-        def weigh_pairs(b):
-            pairs = vector_tile([P, 2, P, 2], BF16)
-            nc.vector.tensor_tensor(
-                pairs[:], looked_up[b, 1][:].rearrange("n (p u e) -> n u p e", u=2, e=2), weight_along, MULT
-            )
-            g_pairs[b] = pairs[:].rearrange("n u p e -> n (u p e)").bitcast(F32)
-
-        def turn_pairs(b):
-            g_bank[b] = bank_tile([P, 2, P])
-            for u in range(2):
-                nc.tensor.transpose(g_bank[b][:, u, :], g_pairs[b][:, rows(u)], ident[:])
-
-        def join(bank, engine):
-            new_tile, copy = engine
+        def join(bank, copy):
             words = new_tile([P, HALF], BF16)
             copy(words[:].bitcast(F32).rearrange("p (c u) -> p c u", u=2), bank.rearrange("p u c -> p c u"))
             return words
-
-        def join_g(b, engine):
-            g_words[b, 1] = join(g_bank[b][:], engine)
 
         def quantize_g(b, h):
             nc.vector.quantize_mx(
@@ -186,8 +159,7 @@ def tile_attend_gvq_cw_w_kernel(tc, zT, cb, tw, xT, offs, out):
         x_codes = {}
         x_scales = {}
 
-        def round_x(j, h, engine):
-            new_tile, copy = engine
+        def round_x(j, h, copy):
             pairs = new_tile([P, 2, P, 2], BF16)
             copy(pairs[:], x_half[j, h].rearrange("d (p u e) -> d u p e", u=2, e=2))
             x_pairs[j, h] = pairs[:].rearrange("d u p e -> d (u p e)").bitcast(F32)
@@ -197,11 +169,11 @@ def tile_attend_gvq_cw_w_kernel(tc, zT, cb, tw, xT, offs, out):
             for u in range(2):
                 nc.tensor.transpose(x_bank[j, h][:, u, :], x_pairs[j, h][:, rows(u)], ident[:])
 
-        def join_x(j, h, engine):
-            x_words[j, h] = join(x_bank[j, h][:], engine)
+        def join_x(j, h, copy):
+            x_words[j, h] = join(x_bank[j, h][:], copy)
 
         def quantize_x(j, h):
-            codes = vector_tile([P, P], U32)
+            codes = new_tile([P, P], U32)
             scales = keep.tile([P, P], U8, name="x_scales%d_%d" % (j, h), align_bytes=ALIGN)
             nc.vector.quantize_mx(out=codes[:].bitcast(E4M3), scales=scales[:], in_=x_words[j, h][:])
             x_codes[j, h] = codes[:]
@@ -210,7 +182,8 @@ def tile_attend_gvq_cw_w_kernel(tc, zT, cb, tw, xT, offs, out):
         sums = {}
 
         def product_pass(j, h):
-            if h == 0:
+            first = j not in sums
+            if first:
                 sums[j] = bank_tile([P, DV])
             nc.tensor.matmul_mx(
                 out=sums[j][:],
@@ -218,14 +191,15 @@ def tile_attend_gvq_cw_w_kernel(tc, zT, cb, tw, xT, offs, out):
                 lhsT_scale=x_scales[j, h],
                 rhs=g_codes[h][:].bitcast(E5M2),
                 rhs_scale=g_scales[h][:],
-                start=h == 0,
-                stop=h == HALVES - 1,
+                start=first,
+                stop=not first,
             )
 
         halves_of_sums = {}
 
         def split_pass(j, h):
-            if h == 0:
+            first = j not in halves_of_sums
+            if first:
                 halves_of_sums[j] = [bank_tile([P, DV // 2]) for side in range(2)]
             for side in range(2):
                 columns = slice(side * DV // 2, (side + 1) * DV // 2)
@@ -235,87 +209,77 @@ def tile_attend_gvq_cw_w_kernel(tc, zT, cb, tw, xT, offs, out):
                     lhsT_scale=x_scales[j, h],
                     rhs=g_codes[h][:, columns].bitcast(E5M2),
                     rhs_scale=g_scales[h][:, columns],
-                    start=h == 0,
-                    stop=h == HALVES - 1,
+                    start=first,
+                    stop=not first,
                 )
 
         def split_store(j, queue):
-            result = vector_tile([P, DV], F32)
+            result = new_tile([P, DV], F32)
             nc.scalar.copy(result[:, : DV // 2], halves_of_sums[j][0][:])
             nc.vector.tensor_copy(result[:, DV // 2 :], halves_of_sums[j][1][:])
             queue.dma_start(out[rows(j), :], result[:])
 
-        def store(j, engine, queue):
-            new_tile, copy = engine
+        def store(j, copy, queue):
             result = new_tile([P, DV], F32)
             copy(result[:], sums[j][:])
             queue.dma_start(out[rows(j), :], result[:])
 
-        held_join = (vector_tile, nc.scalar.copy)
         for b in range(BLOCKS):
-            gather_on_scalar(b)
+            gather_on_vector(b, 0)
+            gather_on_scalar(b, 1)
             if b > 0:
-                turn_pairs(b - 1)
-            if b > 1:
-                weigh_turned(b - 1)
-                quantize_g(b - 1, 0)
-            turn_z(b)
-            turn_c(b)
-            gather_on_vector(b)
-            if b > 0:
-                join_g(b - 1, held_join)
-            if b == 1:
-                weigh_turned(b - 1)
-            if b > 0:
-                quantize_g(b - 1, 1)
-            weigh_pairs(b)
-            if b == 1:
-                quantize_g(b - 1, 0)
+                for h in range(HALVES):
+                    weigh(b - 1, h)
+                for h in range(HALVES):
+                    quantize_g(b - 1, h)
+            for h in range(HALVES):
+                turn_z(b, h)
+            for h in range(HALVES):
+                turn_c(b, h)
         round_x(0, 0, on_scalar)
         round_x(0, 1, on_scalar)
+        weigh(LAST, 0)
         turn_x(0, 0)
-        turn_pairs(LAST)
         turn_x(0, 1)
-        weigh_turned(LAST)
+        weigh(LAST, 1)
         round_x(1, 0, on_scalar)
         round_x(1, 1, on_gpsimd)
-        join_x(0, 0, on_scalar)
-        join_g(LAST, on_scalar)
+        join_x(0, 0, on_vector)
         join_x(0, 1, on_scalar)
-        quantize_g(LAST, 0)
         turn_x(1, 0)
         turn_x(1, 1)
-        quantize_x(0, 0)
-        round_x(2, 0, on_vector)
+        quantize_g(LAST, 0)
         quantize_g(LAST, 1)
+        quantize_x(0, 0)
         quantize_x(0, 1)
         join_x(1, 0, on_scalar)
         join_x(1, 1, on_scalar)
+        round_x(2, 0, on_vector)
         round_x(2, 1, on_vector)
-        quantize_x(1, 0)
         product_pass(0, 0)
         product_pass(0, 1)
-        split_pass(1, 0)
+        round_x(3, 0, on_vector)
+        quantize_x(1, 0)
         turn_x(2, 0)
         turn_x(2, 1)
-        round_x(3, 0, on_vector)
         round_x(3, 1, on_vector)
         quantize_x(1, 1)
         turn_x(3, 0)
-        turn_x(3, 1)
         store(0, on_scalar, nc.sync)
+        split_pass(1, 0)
         split_pass(1, 1)
+        turn_x(3, 1)
         join_x(2, 0, on_vector)
         join_x(2, 1, on_scalar)
         join_x(3, 0, on_vector)
         quantize_x(2, 0)
-        join_x(3, 1, on_scalar)
         quantize_x(2, 1)
         quantize_x(3, 0)
+        split_store(1, nc.sync)
+        join_x(3, 1, on_scalar)
         quantize_x(3, 1)
         for j in (2, 3):
             for h in range(HALVES):
                 split_pass(j, h)
-        split_store(1, nc.sync)
         split_store(2, nc.sync)
         split_store(3, nc.scalar)

@@ -219,6 +219,28 @@ def tile_attend_gvq_cw_w_kernel(tc, zT, cb, tw, xT, offs, out):
             nc.vector.tensor_copy(result[:, DV // 2 :], halves_of_sums[j][1][:])
             queue.dma_start(out[rows(j), :], result[:])
 
+        warm = {}
+
+        def make_warm_up_operand():
+            warm["codes"] = new_tile([P, P], U32)
+            warm["scales"] = keep.tile([P, P], U8, name="warm_scales", align_bytes=ALIGN)
+            nc.vector.quantize_mx(
+                out=warm["codes"][:].bitcast(E4M3),
+                scales=warm["scales"][:],
+                in_=z_half[0, 0][:, : HALF // 2].bitcast(BF16),
+            )
+
+        def warm_up():
+            nc.tensor.matmul_mx(
+                out=bank_tile([P, DV // 2])[:],
+                lhsT=warm["codes"][:].bitcast(E4M3),
+                lhsT_scale=warm["scales"][:],
+                rhs=g_codes[0][:, : DV // 2].bitcast(E5M2),
+                rhs_scale=g_scales[0][:, : DV // 2],
+                start=True,
+                stop=True,
+            )
+
         def store(j, copy, queue):
             result = new_tile([P, DV], F32)
             copy(result[:], sums[j][:])
@@ -227,6 +249,8 @@ def tile_attend_gvq_cw_w_kernel(tc, zT, cb, tw, xT, offs, out):
         for b in range(BLOCKS):
             gather_on_vector(b, 0)
             gather_on_scalar(b, 1)
+            if b == 0:
+                make_warm_up_operand()
             if b > 0:
                 for h in range(HALVES):
                     weigh(b - 1, h)
@@ -244,18 +268,19 @@ def tile_attend_gvq_cw_w_kernel(tc, zT, cb, tw, xT, offs, out):
         weigh(LAST, 1)
         round_x(1, 0, on_scalar)
         round_x(1, 1, on_gpsimd)
-        join_x(0, 0, on_vector)
+        join_x(0, 0, on_scalar)
         join_x(0, 1, on_scalar)
         turn_x(1, 0)
         turn_x(1, 1)
         quantize_g(LAST, 0)
-        quantize_g(LAST, 1)
         quantize_x(0, 0)
+        quantize_g(LAST, 1)
         quantize_x(0, 1)
         join_x(1, 0, on_scalar)
         join_x(1, 1, on_scalar)
         round_x(2, 0, on_vector)
         round_x(2, 1, on_vector)
+        warm_up()
         product_pass(0, 0)
         product_pass(0, 1)
         round_x(3, 0, on_vector)
@@ -265,21 +290,21 @@ def tile_attend_gvq_cw_w_kernel(tc, zT, cb, tw, xT, offs, out):
         round_x(3, 1, on_vector)
         quantize_x(1, 1)
         turn_x(3, 0)
+        turn_x(3, 1)
         store(0, on_scalar, nc.sync)
         split_pass(1, 0)
         split_pass(1, 1)
-        turn_x(3, 1)
         join_x(2, 0, on_vector)
         join_x(2, 1, on_scalar)
         join_x(3, 0, on_vector)
         quantize_x(2, 0)
+        join_x(3, 1, on_scalar)
         quantize_x(2, 1)
         quantize_x(3, 0)
-        split_store(1, nc.sync)
-        join_x(3, 1, on_scalar)
         quantize_x(3, 1)
         for j in (2, 3):
             for h in range(HALVES):
                 split_pass(j, h)
+        split_store(1, nc.sync)
         split_store(2, nc.sync)
         split_store(3, nc.scalar)

@@ -219,28 +219,6 @@ def tile_attend_gvq_cw_w_kernel(tc, zT, cb, tw, xT, offs, out):
             nc.vector.tensor_copy(result[:, DV // 2 :], halves_of_sums[j][1][:])
             queue.dma_start(out[rows(j), :], result[:])
 
-        warm = {}
-
-        def make_warm_up_operand():
-            warm["codes"] = new_tile([P, P], U32)
-            warm["scales"] = keep.tile([P, P], U8, name="warm_scales", align_bytes=ALIGN)
-            nc.vector.quantize_mx(
-                out=warm["codes"][:].bitcast(E4M3),
-                scales=warm["scales"][:],
-                in_=z_half[0, 0][:, : HALF // 2].bitcast(BF16),
-            )
-
-        def warm_up():
-            nc.tensor.matmul_mx(
-                out=bank_tile([P, DV // 2])[:],
-                lhsT=warm["codes"][:].bitcast(E4M3),
-                lhsT_scale=warm["scales"][:],
-                rhs=g_codes[0][:, : DV // 2].bitcast(E5M2),
-                rhs_scale=g_scales[0][:, : DV // 2],
-                start=True,
-                stop=True,
-            )
-
         def store(j, copy, queue):
             result = new_tile([P, DV], F32)
             copy(result[:], sums[j][:])
@@ -249,8 +227,6 @@ def tile_attend_gvq_cw_w_kernel(tc, zT, cb, tw, xT, offs, out):
         for b in range(BLOCKS):
             gather_on_vector(b, 0)
             gather_on_scalar(b, 1)
-            if b == 0:
-                make_warm_up_operand()
             if b > 0:
                 for h in range(HALVES):
                     weigh(b - 1, h)
@@ -280,7 +256,6 @@ def tile_attend_gvq_cw_w_kernel(tc, zT, cb, tw, xT, offs, out):
         join_x(1, 1, on_scalar)
         round_x(2, 0, on_vector)
         round_x(2, 1, on_vector)
-        warm_up()
         product_pass(0, 0)
         product_pass(0, 1)
         round_x(3, 0, on_vector)

@@ -45,7 +45,9 @@ def tile_attend_gvq_cw_w_kernel(tc, zT, cb, tw, xT, offs, out):
 
         on_vector = nc.vector.tensor_copy
         on_scalar = nc.scalar.copy
-        on_gpsimd = nc.gpsimd.tensor_copy
+
+        def on_gpsimd(result, source):
+            nc.gpsimd.tensor_scalar(result, source, 1.0, 0.0, MULT, ADD)
 
         def rows(i):
             return slice(i * P, (i + 1) * P)
@@ -58,9 +60,14 @@ def tile_attend_gvq_cw_w_kernel(tc, zT, cb, tw, xT, offs, out):
         z_half = {}
         x_half = {}
 
+        def features(source, b):
+            if b < 2:
+                return source[0 : 2 * P, :].rearrange("(p j) c -> j p c", j=2)[b]
+            return source[rows(b), :]
+
         def load_codebook(b):
             codebook[b] = keep.tile([P, C], F32, name="cb%d" % b)
-            nc.sync.dma_start(codebook[b][:], cb[rows(b), :])
+            nc.sync.dma_start(codebook[b][:], features(cb, b))
 
         def load_whole(source, name, i, halves):
             whole = keep.tile([P, T], F32, name="%s%d" % (name, i))
@@ -78,9 +85,15 @@ def tile_attend_gvq_cw_w_kernel(tc, zT, cb, tw, xT, offs, out):
         load_codebook(0)
         nc.sync.dma_start(tw_rows[0:HALVES, :], tw[0:1, :].rearrange("o (h t) -> (o h) t", h=HALVES))
         nc.sync.dma_start(offsets[:], offs)
-        for b in range(LAST):
-            load_whole(zT, "z", b, z_half)
-            load_codebook(b + 1)
+        z_pair = keep.tile([P, 2, T], F32, name="z_pair")
+        nc.sync.dma_start(z_pair[:], zT[0 : 2 * P, :].rearrange("(p j) t -> p j t", j=2))
+        for b in range(2):
+            for h in range(HALVES):
+                z_half[b, h] = z_pair[:, b, tokens(h)]
+        load_codebook(1)
+        load_codebook(2)
+        load_whole(zT, "z", 2, z_half)
+        load_codebook(LAST)
         for h in range(HALVES):
             load_half(zT, "z", LAST, h, z_half)
         for j in range(LAST):
@@ -154,6 +167,7 @@ def tile_attend_gvq_cw_w_kernel(tc, zT, cb, tw, xT, offs, out):
             )
 
         x_pairs = {}
+        x_part = {}
         x_bank = {}
         x_words = {}
         x_codes = {}
@@ -163,6 +177,16 @@ def tile_attend_gvq_cw_w_kernel(tc, zT, cb, tw, xT, offs, out):
             pairs = new_tile([P, 2, P, 2], BF16)
             copy(pairs[:], x_half[j, h].rearrange("d (p u e) -> d u p e", u=2, e=2))
             x_pairs[j, h] = pairs[:].rearrange("d u p e -> d (u p e)").bitcast(F32)
+
+        def round_part(j, h, u, copy):
+            pairs = new_tile([P, P, 2], BF16)
+            copy(pairs[:], x_half[j, h].rearrange("d (p u e) -> d u p e", u=2, e=2)[:, u])
+            x_part[j, h, u] = pairs[:].rearrange("d p e -> d (p e)").bitcast(F32)
+
+        def turn_part(j, h, u):
+            if (j, h) not in x_bank:
+                x_bank[j, h] = bank_tile([P, 2, P])
+            nc.tensor.transpose(x_bank[j, h][:, u, :], x_part[j, h, u], ident[:])
 
         def turn_x(j, h):
             x_bank[j, h] = bank_tile([P, 2, P])
@@ -213,48 +237,67 @@ def tile_attend_gvq_cw_w_kernel(tc, zT, cb, tw, xT, offs, out):
                     stop=not first,
                 )
 
+        def undeal(result, left):
+            nc.scalar.copy(
+                result[:, : DV // 2].rearrange("d (p b) -> d p b", b=2), left.rearrange("d (b p) -> d p b", b=2)
+            )
+
         def split_store(j, queue):
             result = new_tile([P, DV], F32)
-            nc.scalar.copy(result[:, : DV // 2], halves_of_sums[j][0][:])
+            undeal(result, halves_of_sums[j][0][:])
             nc.vector.tensor_copy(result[:, DV // 2 :], halves_of_sums[j][1][:])
             queue.dma_start(out[rows(j), :], result[:])
 
         def store(j, copy, queue):
             result = new_tile([P, DV], F32)
-            copy(result[:], sums[j][:])
+            undeal(result, sums[j][:, : DV // 2])
+            copy(result[:, DV // 2 :], sums[j][:, DV // 2 :])
             queue.dma_start(out[rows(j), :], result[:])
 
-        for b in range(BLOCKS):
+        gather_on_vector(0, 0)
+        gather_on_scalar(0, 1)
+        turn_c(0, 0)
+        turn_z(0, 0)
+        turn_z(0, 1)
+        turn_c(0, 1)
+        weigh(0, 0)
+        for b in range(1, BLOCKS):
             gather_on_vector(b, 0)
             gather_on_scalar(b, 1)
-            if b > 0:
-                for h in range(HALVES):
+            for h in range(HALVES):
+                if (b - 1, h) not in g_words:
                     weigh(b - 1, h)
-                for h in range(HALVES):
-                    quantize_g(b - 1, h)
+            for h in range(HALVES):
+                quantize_g(b - 1, h)
             for h in range(HALVES):
                 turn_z(b, h)
             for h in range(HALVES):
                 turn_c(b, h)
-        round_x(0, 0, on_scalar)
-        round_x(0, 1, on_scalar)
+        for u in range(2):
+            round_part(0, 0, u, on_scalar)
+        for u in range(2):
+            round_part(0, 1, u, on_scalar)
         weigh(LAST, 0)
-        turn_x(0, 0)
-        turn_x(0, 1)
+        for u in range(2):
+            turn_part(0, 0, u)
+        for u in range(2):
+            turn_part(0, 1, u)
         weigh(LAST, 1)
-        round_x(1, 0, on_scalar)
+        round_part(1, 0, 0, on_scalar)
         round_x(1, 1, on_gpsimd)
         join_x(0, 0, on_scalar)
+        round_part(1, 0, 1, on_scalar)
         join_x(0, 1, on_scalar)
-        turn_x(1, 0)
+        turn_part(1, 0, 0)
         turn_x(1, 1)
+        turn_part(1, 0, 1)
         quantize_g(LAST, 0)
         quantize_x(0, 0)
         quantize_g(LAST, 1)
         quantize_x(0, 1)
-        join_x(1, 0, on_scalar)
-        join_x(1, 1, on_scalar)
         round_x(2, 0, on_vector)
+        join_x(1, 1, on_scalar)
+        join_x(1, 0, on_scalar)
         round_x(2, 1, on_vector)
         product_pass(0, 0)
         product_pass(0, 1)
@@ -276,10 +319,10 @@ def tile_attend_gvq_cw_w_kernel(tc, zT, cb, tw, xT, offs, out):
         join_x(3, 1, on_scalar)
         quantize_x(2, 1)
         quantize_x(3, 0)
+        split_store(1, nc.sync)
         quantize_x(3, 1)
         for j in (2, 3):
             for h in range(HALVES):
                 split_pass(j, h)
-        split_store(1, nc.sync)
         split_store(2, nc.sync)
         split_store(3, nc.scalar)

@@ -45,9 +45,7 @@ def tile_attend_gvq_cw_w_kernel(tc, zT, cb, tw, xT, offs, out):
 
         on_vector = nc.vector.tensor_copy
         on_scalar = nc.scalar.copy
-
-        def on_gpsimd(result, source):
-            nc.gpsimd.tensor_scalar(result, source, 1.0, 0.0, MULT, ADD)
+        on_gpsimd = nc.gpsimd.tensor_copy
 
         def rows(i):
             return slice(i * P, (i + 1) * P)
@@ -96,8 +94,10 @@ def tile_attend_gvq_cw_w_kernel(tc, zT, cb, tw, xT, offs, out):
         load_codebook(LAST)
         for h in range(HALVES):
             load_half(zT, "z", LAST, h, z_half)
-        for j in range(LAST):
-            load_whole(xT, "x", j, x_half)
+        load_whole(xT, "x", 0, x_half)
+        for h in range(HALVES):
+            load_half(xT, "x", 1, h, x_half)
+        load_whole(xT, "x", 2, x_half)
         for h in range(HALVES):
             load_half(xT, "x", LAST, h, x_half)
 
@@ -273,31 +273,27 @@ def tile_attend_gvq_cw_w_kernel(tc, zT, cb, tw, xT, offs, out):
                 turn_z(b, h)
             for h in range(HALVES):
                 turn_c(b, h)
-        for u in range(2):
-            round_part(0, 0, u, on_scalar)
-        for u in range(2):
-            round_part(0, 1, u, on_scalar)
+        round_x(0, 0, on_scalar)
+        round_x(0, 1, on_scalar)
         weigh(LAST, 0)
-        for u in range(2):
-            turn_part(0, 0, u)
-        for u in range(2):
-            turn_part(0, 1, u)
+        turn_x(0, 0)
+        turn_x(0, 1)
         weigh(LAST, 1)
-        round_part(1, 0, 0, on_scalar)
-        round_x(1, 1, on_gpsimd)
+        round_x(1, 0, on_gpsimd)
+        round_part(1, 1, 0, on_scalar)
         join_x(0, 0, on_scalar)
-        round_part(1, 0, 1, on_scalar)
+        round_part(1, 1, 1, on_scalar)
         join_x(0, 1, on_scalar)
-        turn_part(1, 0, 0)
-        turn_x(1, 1)
-        turn_part(1, 0, 1)
+        turn_part(1, 1, 0)
+        turn_x(1, 0)
+        turn_part(1, 1, 1)
         quantize_g(LAST, 0)
         quantize_x(0, 0)
         quantize_g(LAST, 1)
         quantize_x(0, 1)
         round_x(2, 0, on_vector)
-        join_x(1, 1, on_scalar)
         join_x(1, 0, on_scalar)
+        join_x(1, 1, on_scalar)
         round_x(2, 1, on_vector)
         product_pass(0, 0)
         product_pass(0, 1)

from contextlib import ExitStack

import concourse.mybir as mybir
from concourse.masks import make_identity

T, C, D, DV = 1024, 2048, 512, 512
BETA = 0.25
FLOPS = 2 * T * D * DV

F32 = mybir.dt.float32
BF16 = mybir.dt.bfloat16
U32 = mybir.dt.uint32
U16 = mybir.dt.uint16
U8 = mybir.dt.uint8
E4M3 = mybir.dt.float8_e4m3fn_x4
E5M2 = mybir.dt.float8_e5m2_x4
MULT = mybir.AluOpType.mult
ADD = mybir.AluOpType.add
COPY = mybir.ActivationFunctionType.Copy

P = 128
SLOTS = 4
HALF = P * SLOTS
HALVES = T // HALF
LIST_COLS = HALF // 16
BLOCKS = 4
LAST = BLOCKS - 1
PSUM_BANKS = 8
ALIGN = 64
RING_BUFFERS = 64


def tile_attend_gvq_cw_w_kernel(tc, zT, cb, tw, xT, offs, out):
    nc = tc.nc
    with ExitStack() as ctx:
        keep = ctx.enter_context(tc.tile_pool(name="keep", bufs=1))
        psum = ctx.enter_context(tc.psum_pool(name="psum", bufs=PSUM_BANKS))
        ring = ctx.enter_context(tc.tile_pool(name="ring", bufs=RING_BUFFERS))

        def new_tile(shape, dtype):
            return ring.tile(shape, dtype, name="made", tag="made", align_bytes=ALIGN)

        def bank_tile(shape):
            return psum.tile(shape, F32, name="bank", tag="bank")

        on_vector = nc.vector.tensor_copy
        on_scalar = nc.scalar.copy
        on_gpsimd = nc.gpsimd.tensor_copy

        def rows(i):
            return slice(i * P, (i + 1) * P)

        def tokens(h):
            return slice(h * HALF, (h + 1) * HALF)

        offsets = keep.tile([P, T // 16], U16, name="offsets")
        codebook = {}
        z_half = {}
        x_half = {}

        def features(source, b):
            if b < 2:
                return source[0 : 2 * P, :].rearrange("(p j) c -> j p c", j=2)[b]
            return source[rows(b), :]

        def load_codebook(b):
            codebook[b] = keep.tile([P, C], F32, name="cb%d" % b)
            nc.sync.dma_start(codebook[b][:], features(cb, b))

        def load_whole(source, name, i, halves):
            whole = keep.tile([P, T], F32, name="%s%d" % (name, i))
            nc.sync.dma_start(whole[:], source[rows(i), :])
            for h in range(HALVES):
                halves[i, h] = whole[:, tokens(h)]

        def load_half(source, name, i, h, halves):
            part = keep.tile([P, HALF], F32, name="%s%d_%d" % (name, i, h))
            nc.sync.dma_start(part[:], source[rows(i), tokens(h)])
            halves[i, h] = part[:]

        tw_rows = keep.tile([P, HALF], F32, name="tw_rows")
        nc.vector.memset(tw_rows[:], 0.0)
        load_codebook(0)
        nc.sync.dma_start(tw_rows[0:HALVES, :], tw[0:1, :].rearrange("o (h t) -> (o h) t", h=HALVES))
        nc.sync.dma_start(offsets[:], offs)
        z_pair = keep.tile([P, 2, T], F32, name="z_pair")
        nc.sync.dma_start(z_pair[:], zT[0 : 2 * P, :].rearrange("(p j) t -> p j t", j=2))
        for b in range(2):
            for h in range(HALVES):
                z_half[b, h] = z_pair[:, b, tokens(h)]
        load_codebook(1)
        load_codebook(2)
        load_whole(zT, "z", 2, z_half)
        load_codebook(LAST)
        for h in range(HALVES):
            load_half(zT, "z", LAST, h, z_half)
        load_whole(xT, "x", 0, x_half)
        for h in range(HALVES):
            load_half(xT, "x", 1, h, x_half)
        load_whole(xT, "x", 2, x_half)
        for h in range(HALVES):
            load_half(xT, "x", LAST, h, x_half)

        ident = keep.tile([P, P], F32, name="ident")
        make_identity(nc, ident[:])

        tw_bank = bank_tile([P, SLOTS, P])
        for s in range(SLOTS):
            nc.tensor.transpose(tw_bank[:, s, :], tw_rows[:, s:HALF:SLOTS], ident[:])
        weight = new_tile([P, HALVES, SLOTS], F32)
        nc.scalar.activation(weight[:], tw_bank[:, :, 0:HALVES].rearrange("p s h -> p h s"), COPY, scale=BETA)

        g_codes = [keep.tile([P, DV], U32, name="g_codes%d" % h, align_bytes=ALIGN) for h in range(HALVES)]
        g_scales = [keep.tile([P, DV], U8, name="g_scales%d" % h, align_bytes=ALIGN) for h in range(HALVES)]
        e_bank = {}
        minus_c = {}
        g_words = {}

        def listed(b, h):
            return codebook[b][:].indirect(offsets[:, h * LIST_COLS : (h + 1) * LIST_COLS])

        def gather_on_vector(b, h):
            minus_c[b, h] = new_tile([P, HALF], F32)
            nc.vector.tensor_scalar(minus_c[b, h][:], listed(b, h), -1.0, 0.0, MULT, ADD)

        def gather_on_scalar(b, h):
            minus_c[b, h] = new_tile([P, HALF], F32)
            nc.scalar.activation(minus_c[b, h][:], listed(b, h), COPY, scale=-1.0)

        def add_turned(b, h, source):
            first = (b, h) not in e_bank
            if first:
                e_bank[b, h] = bank_tile([P, SLOTS, P])
            for s in range(SLOTS):
                nc.tensor.matmul(
                    e_bank[b, h][:, s, :],
                    lhsT=source[:, s:HALF:SLOTS],
                    rhs=ident[:],
                    is_transpose=True,
                    start=first and s == 0,
                    stop=not first and s == SLOTS - 1,
                )

        def turn_z(b, h):
            add_turned(b, h, z_half[b, h])

        def turn_c(b, h):
            add_turned(b, h, minus_c[b, h][:])

        def weigh(b, h):
            g_words[b, h] = new_tile([P, HALF], BF16)
            nc.vector.tensor_tensor(
                g_words[b, h][:].rearrange("p (n s) -> p n s", s=SLOTS),
                e_bank[b, h][:].rearrange("p s n -> p n s"),
                weight[:, h, :].unsqueeze(1).to_broadcast([P, P, SLOTS]),
                MULT,
            )

        def join(bank, copy):
            words = new_tile([P, HALF], BF16)
            copy(words[:].bitcast(F32).rearrange("p (c u) -> p c u", u=2), bank.rearrange("p u c -> p c u"))
            return words

        def quantize_g(b, h):
            nc.vector.quantize_mx(
                out=g_codes[h][:, rows(b)].bitcast(E5M2), scales=g_scales[h][:, rows(b)], in_=g_words[b, h][:]
            )

        x_pairs = {}
        x_part = {}
        x_bank = {}
        x_words = {}
        x_codes = {}
        x_scales = {}

        def round_x(j, h, copy):
            pairs = new_tile([P, 2, P, 2], BF16)
            copy(pairs[:], x_half[j, h].rearrange("d (p u e) -> d u p e", u=2, e=2))
            x_pairs[j, h] = pairs[:].rearrange("d u p e -> d (u p e)").bitcast(F32)

        def round_part(j, h, u, copy):
            pairs = new_tile([P, P, 2], BF16)
            copy(pairs[:], x_half[j, h].rearrange("d (p u e) -> d u p e", u=2, e=2)[:, u])
            x_part[j, h, u] = pairs[:].rearrange("d p e -> d (p e)").bitcast(F32)

        def turn_part(j, h, u):
            if (j, h) not in x_bank:
                x_bank[j, h] = bank_tile([P, 2, P])
            nc.tensor.transpose(x_bank[j, h][:, u, :], x_part[j, h, u], ident[:])

        def turn_x(j, h):
            x_bank[j, h] = bank_tile([P, 2, P])
            for u in range(2):
                nc.tensor.transpose(x_bank[j, h][:, u, :], x_pairs[j, h][:, rows(u)], ident[:])

        def join_x(j, h, copy):
            x_words[j, h] = join(x_bank[j, h][:], copy)

        def quantize_x(j, h):
            codes = new_tile([P, P], U32)
            scales = keep.tile([P, P], U8, name="x_scales%d_%d" % (j, h), align_bytes=ALIGN)
            nc.vector.quantize_mx(out=codes[:].bitcast(E4M3), scales=scales[:], in_=x_words[j, h][:])
            x_codes[j, h] = codes[:]
            x_scales[j, h] = scales[:]

        sums = {}

        def product_pass(j, h):
            first = j not in sums
            if first:
                sums[j] = bank_tile([P, DV])
            nc.tensor.matmul_mx(
                out=sums[j][:],
                lhsT=x_codes[j, h].bitcast(E4M3),
                lhsT_scale=x_scales[j, h],
                rhs=g_codes[h][:].bitcast(E5M2),
                rhs_scale=g_scales[h][:],
                start=first,
                stop=not first,
            )

        halves_of_sums = {}

        def split_pass(j, h):
            first = j not in halves_of_sums
            if first:
                halves_of_sums[j] = [bank_tile([P, DV // 2]) for side in range(2)]
            for side in range(2):
                columns = slice(side * DV // 2, (side + 1) * DV // 2)
                nc.tensor.matmul_mx(
                    out=halves_of_sums[j][side][:],
                    lhsT=x_codes[j, h].bitcast(E4M3),
                    lhsT_scale=x_scales[j, h],
                    rhs=g_codes[h][:, columns].bitcast(E5M2),
                    rhs_scale=g_scales[h][:, columns],
                    start=first,
                    stop=not first,
                )

        def undeal(result, left):
            nc.scalar.copy(
                result[:, : DV // 2].rearrange("d (p b) -> d p b", b=2), left.rearrange("d (b p) -> d p b", b=2)
            )

        def split_store(j, queue):
            result = new_tile([P, DV], F32)
            undeal(result, halves_of_sums[j][0][:])
            nc.vector.tensor_copy(result[:, DV // 2 :], halves_of_sums[j][1][:])
            queue.dma_start(out[rows(j), :], result[:])

        def store(j, copy, queue):
            result = new_tile([P, DV], F32)
            undeal(result, sums[j][:, : DV // 2])
            copy(result[:, DV // 2 :], sums[j][:, DV // 2 :])
            queue.dma_start(out[rows(j), :], result[:])

        gather_on_vector(0, 0)
        gather_on_scalar(0, 1)
        turn_c(0, 0)
        turn_z(0, 0)
        turn_z(0, 1)
        turn_c(0, 1)
        weigh(0, 0)
        for b in range(1, BLOCKS):
            gather_on_vector(b, 0)
            gather_on_scalar(b, 1)
            for h in range(HALVES):
                if (b - 1, h) not in g_words:
                    weigh(b - 1, h)
            for h in range(HALVES):
                quantize_g(b - 1, h)
            for h in range(HALVES):
                turn_z(b, h)
            for h in range(HALVES):
                turn_c(b, h)
        round_x(0, 0, on_scalar)
        round_x(0, 1, on_scalar)
        weigh(LAST, 0)
        turn_x(0, 0)
        turn_x(0, 1)
        weigh(LAST, 1)
        round_x(1, 0, on_gpsimd)
        round_part(1, 1, 0, on_scalar)
        join_x(0, 0, on_scalar)
        round_part(1, 1, 1, on_scalar)
        join_x(0, 1, on_scalar)
        turn_part(1, 1, 0)
        turn_x(1, 0)
        turn_part(1, 1, 1)
        quantize_g(LAST, 0)
        quantize_x(0, 0)
        quantize_g(LAST, 1)
        quantize_x(0, 1)
        round_x(2, 0, on_vector)
        join_x(1, 0, on_scalar)
        join_x(1, 1, on_scalar)
        round_x(2, 1, on_vector)
        product_pass(0, 0)
        product_pass(0, 1)
        round_x(3, 0, on_vector)
        quantize_x(1, 0)
        turn_x(2, 0)
        turn_x(2, 1)
        round_x(3, 1, on_vector)
        quantize_x(1, 1)
        turn_x(3, 0)
        turn_x(3, 1)
        store(0, on_scalar, nc.sync)
        split_pass(1, 0)
        split_pass(1, 1)
        join_x(2, 0, on_vector)
        join_x(2, 1, on_scalar)
        join_x(3, 0, on_vector)
        quantize_x(2, 0)
        join_x(3, 1, on_scalar)
        quantize_x(2, 1)
        quantize_x(3, 0)
        split_store(1, nc.sync)
        quantize_x(3, 1)
        for j in (2, 3):
            for h in range(HALVES):
                split_pass(j, h)
        split_store(2, nc.sync)
        split_store(3, nc.scalar)
